import numpy as np
import ml_dtypes


def mxq(x, axis, fmt="e4m3"):
    dtype, down = {"e4m3": (ml_dtypes.float8_e4m3fn, 7), "e5m2": (ml_dtypes.float8_e5m2, 14)}[fmt]
    v = np.moveaxis(np.asarray(x, np.float32).astype(ml_dtypes.bfloat16).astype(np.float64), axis, -1)
    blocks = v.reshape(v.shape[:-1] + (-1, 32))
    amax = np.abs(blocks).max(-1, keepdims=True)
    byte = np.maximum(np.where(amax > 0, np.frexp(amax)[1] - 1 + 127, 0) - down, 1)
    scale = np.exp2(byte - 127.0)
    codes = (blocks / scale).astype(np.float32).astype(dtype).astype(np.float64)
    return np.moveaxis((codes * scale).reshape(v.shape), -1, axis)


WIDE = False


def mx_kscale(k):
    if not WIDE:
        return np.ones(k)
    levels = np.array([30, -30])
    if k % 512:
        return np.exp2(np.random.permutation(np.resize(levels, k // 32))).repeat(32)
    a = np.empty((k // 512, 16))
    for p in range(k // 512):
        a[p, :8] = np.random.permutation(np.resize(levels, 8))
        for g in range(8):
            far = levels[np.abs(levels - a[p, g]) >= 10]
            a[p, g + 8] = far[np.random.randint(len(far))]
    return np.exp2(a.ravel()).repeat(32)


def f64(x):
    return np.asarray(x).astype(np.float64)


def striped(idx):
    return np.tile(idx.reshape(-1, 16).T, (8, 1)).astype(np.uint16)


def unstriped(offs):
    return offs[:16].T.reshape(-1).astype(np.int64)


E2M1 = np.array([0.0, 0.5, 1.0, 1.5, 2.0, 3.0, 4.0, 6.0, -0.0, -0.5, -1.0, -1.5, -2.0, -3.0, -4.0, -6.0])


def pack_weight(w, fmt):
    k, n = w.shape
    w = f64(np.asarray(w, np.float32).astype(ml_dtypes.bfloat16)).reshape(k // 32, 32, n)
    amax = np.abs(w).max(1)
    if fmt == "e4m3":
        byte = np.frexp(amax)[1] - 1 + 127 - 7
    elif fmt == "e5m2":
        byte = np.frexp(amax)[1] - 1 + 127 - 14
    else:
        mant, ex = np.frexp(amax / 6.0)
        byte = np.where(mant > 0.5, ex, ex - 1) + 127
    byte = np.clip(np.where(amax > 0, byte, 1), 1, 254)
    scaled = (w * np.exp2(127.0 - byte)[:, None, :]).reshape(k, n).astype(np.float32)
    by_word = np.ascontiguousarray(scaled.reshape(k // 512, 128, 4, n).transpose(0, 1, 3, 2))
    if fmt == "e4m3":
        words = by_word.astype(ml_dtypes.float8_e4m3fn).view(np.uint8)
    elif fmt == "e5m2":
        words = by_word.astype(ml_dtypes.float8_e5m2).view(np.uint8)
    else:
        c = by_word.astype(ml_dtypes.float4_e2m1fn).view(np.uint8) & 0xF
        words = (c[..., 0::2] | (c[..., 1::2] << 4)).reshape(k // 512, 128, 2 * n)
    return np.ascontiguousarray(words), np.ascontiguousarray(byte.astype(np.uint8).reshape(k // 512, 16, n))


def unpack_weight(words, scales, fmt):
    g, _, n = scales.shape
    words = np.ascontiguousarray(words).reshape(g, 128, n, -1)
    if fmt == "e4m3":
        vals = words.view(ml_dtypes.float8_e4m3fn).astype(np.float64)
    elif fmt == "e5m2":
        vals = words.view(ml_dtypes.float8_e5m2).astype(np.float64)
    else:
        nib = np.empty((g, 128, n, 4), np.uint8)
        nib[..., 0::2] = words & 0xF
        nib[..., 1::2] = words >> 4
        vals = E2M1[nib]
    vals = vals * np.repeat(np.exp2(scales.astype(np.float64) - 127.0), 8, axis=1)[..., None]
    return vals.transpose(0, 1, 3, 2).reshape(g * 512, n)


def d_relu2(v):
    return 2.0 * np.maximum(v, 0.0)


K, T, E, C, H, N = 256, 1024, 2, 512, 512, 512


def by_expert(wq, xq):
    return np.concatenate([wq[e].T @ xq[:, e * C:(e + 1) * C] for e in range(E)], axis=1)


def setup_inputs():
    n = np.random.standard_normal
    v = mx_kscale(N)
    u = mx_kscale(H)
    slot_token = np.random.permutation(T)[:E * C]
    dy = pack_weight(n((N, T)) * v[:, None], "e5m2")
    w2t = [pack_weight(m, "e2m1") for m in n((E, N, H)) / np.sqrt(N) / v[None, :, None] * u]
    return {
        "dy_words": dy[0],
        "dy_scales": dy[1],
        "w2t_words": np.stack([m[0] for m in w2t]),
        "w2t_scales": np.stack([m[1] for m in w2t]),
        "w1t": (n((H, K)) / np.sqrt(H) / u[:, None]).astype(np.float32),
        "a": (n((H, T))).astype(np.float32),
        "gate": np.tile(np.random.uniform(0.2, 1.0, E * C), (128, 1)).astype(np.float32),
        "offs": striped(slot_token),
    }


def reference(dy_words, dy_scales, w2t_words, w2t_scales, w1t, a, gate, offs):
    w2t = np.stack([unpack_weight(w2t_words[e], w2t_scales[e], "e2m1") for e in range(E)])
    w1tq = mxq(f64(w1t), 0, "e4m3")
    idx = unstriped(offs)
    gq = unpack_weight(dy_words, dy_scales, "e5m2")[:, idx]
    y = by_expert(w2t, gq)
    dh = np.zeros((H, T))
    dh[:, idx] = f64(gate[:1]) * y
    return w1tq.T @ mxq(dh * d_relu2(f64(a)), 0, "e5m2")

@@ -1,0 +1,178 @@
+from contextlib import ExitStack
+
+import concourse.mybir as mybir
+from concourse.masks import make_identity
+
+K, T, E, C, H, N = 256, 1024, 2, 512, 512, 512
+FLOPS = 2 * N * H * E * C + 2 * H * K * T
+
+F32 = mybir.dt.float32
+BF16 = mybir.dt.bfloat16
+I32 = mybir.dt.int32
+U32 = mybir.dt.uint32
+U16 = mybir.dt.uint16
+U8 = mybir.dt.uint8
+E4M3 = mybir.dt.float8_e4m3fn_x4
+E5M2 = mybir.dt.float8_e5m2_x4
+E2M1 = mybir.dt.float4_e2m1fn_x4
+MULT = mybir.AluOpType.mult
+COPY = mybir.ActivationFunctionType.Copy
+RELU = mybir.ActivationFunctionType.Relu
+
+P = 128
+PACK = 4
+HALF = 512
+
+
+def tile_moe_sub_relu2_kernel(
+    tc, dy_words, dy_scales, w2t_words, w2t_scales, w1t, a, gate, offs, out
+):
+    nc = tc.nc
+    with ExitStack() as ctx:
+        keep = ctx.enter_context(tc.tile_pool(name="keep", bufs=1))
+        psum = ctx.enter_context(tc.psum_pool(name="psum", bufs=1))
+
+        offsets = keep.tile([P, T // 16], U16, name="offsets")
+        dy_w = keep.tile([P, T], I32, name="dy_w", align_bytes=64)
+        dy_s = keep.tile([P, T // 4], I32, name="dy_s", align_bytes=64)
+        w2_w = keep.tile([P, E, 2 * H], U8, name="w2_w", align_bytes=64)
+        w2_s = keep.tile([P, E, H // 4], I32, name="w2_s", align_bytes=64)
+        gate_rows = keep.tile([P, P], F32, name="gate_rows")
+        ident = keep.tile([P, P], F32, name="ident")
+
+        nc.vector.memset(dy_s[:], 0)
+        nc.vector.memset(w2_s[:], 0)
+        make_identity(nc, ident[:])
+
+        nc.sync.dma_start(offsets[:], offs)
+        nc.sync.dma_start(dy_w[:], dy_words[0].rearrange("p t d -> p (t d)").bitcast(I32))
+        dys32 = dy_scales[0].bitcast(I32)
+        for q in range(4):
+            nc.sync.dma_start(dy_s[32 * q : 32 * q + 4, :], dys32[4 * q : 4 * q + 4, :])
+        nc.sync.dma_start(gate_rows[:], gate[0:16, :].rearrange("r (b c) -> (r b) c", c=P))
+        nc.sync.dma_start(w2_w[:].bitcast(I32), w2t_words[:, 0].rearrange("e p b -> p e b").bitcast(I32))
+        w2s32 = w2t_scales[:, 0].rearrange("e b i -> b e i").bitcast(I32)
+        for q in range(4):
+            nc.sync.dma_start(w2_s[32 * q : 32 * q + 4, :, :], w2s32[4 * q : 4 * q + 4, :, :])
+        a_rows = a.rearrange("(p r) t -> p r t", r=PACK)
+        a_sb = []
+        for r in range(PACK):
+            a_r = keep.tile([P, T], F32, name="a%d" % r)
+            a_sb.append(a_r)
+        w1_raw = keep.tile([P, PACK, K], F32, name="w1_raw")
+        for r in (1, 2, 3, 0):
+            nc.sync.dma_start(a_sb[r][:], a_rows[:, r, :])
+        nc.sync.dma_start(w1_raw[:], w1t.rearrange("(p r) k -> p r k", r=PACK))
+
+        g_w = keep.tile([P, T], U32, name="g_w", align_bytes=64)
+        g_s = keep.tile([P, T], U8, name="g_s", align_bytes=64)
+        for lo, hi in ((0, 256), (256, 512), (512, 1024)):
+            cols = offsets[:, lo // 16 : hi // 16]
+            nc.vector.tensor_copy(g_w[:, lo:hi], dy_w[:].bitcast(U32).indirect(cols))
+            nc.vector.tensor_copy(g_s[:, lo:hi], dy_s[:].bitcast(U8).indirect(cols))
+
+        gate_ps = psum.tile([P, P], F32, name="gate_ps")
+        nc.tensor.transpose(gate_ps[:], gate_rows[:], ident[:])
+        gate2 = keep.tile([P, 8], F32, name="gate2")
+        nc.scalar.activation(gate2[:], gate_ps[:, 0:8], COPY, scale=2.0)
+
+        y_t = [keep.tile([P, PACK, P], F32, name="y_t%d" % j) for j in range(8)]
+        y_s = [[keep.tile([P, C], F32, name="y_s%d_%d" % (r, e)) for e in range(E)] for r in range(PACK)]
+        dh = [keep.tile([P, T], F32, name="dh%d" % r) for r in range(PACK)]
+        da = keep.tile([P, T, PACK], BF16, name="da", align_bytes=64)
+
+        def product(j):
+            e = j // 4
+            acc = psum.tile([P, H], F32, name="acc", tag="acc", bufs=4)
+            nc.tensor.matmul_mx(
+                out=acc[:],
+                lhsT=g_w[:, j * P : (j + 1) * P].bitcast(E5M2),
+                lhsT_scale=g_s[:, j * P : (j + 1) * P],
+                rhs=w2_w[:, e, :].bitcast(E2M1),
+                rhs_scale=w2_s[:, e, :].bitcast(U8),
+                start=True,
+                stop=True,
+            )
+            nc.scalar.activation(
+                y_t[j][:], acc[:].rearrange("p (m r) -> p r m", r=PACK), COPY, scale=gate2[:, j : j + 1]
+            )
+
+        def turn(r, e, blocks):
+            bank = psum.tile([P, C], F32, name="bank", tag="bank", bufs=3)
+            for b in blocks:
+                nc.tensor.transpose(bank[:, b * P : (b + 1) * P], y_t[4 * e + b][:, r, :], ident[:])
+            lo, hi = blocks[0] * P, (blocks[-1] + 1) * P
+            nc.scalar.copy(y_s[r][e][:, lo:hi], bank[:, lo:hi])
+
+        def scatter(r, e, lo, hi):
+            cols = offsets[:, (e * C + lo) // 16 : (e * C + hi) // 16]
+            nc.vector.tensor_copy(dh[r][:].indirect(cols), y_s[r][e][:, lo:hi])
+
+        def relu(r):
+            ra = keep.tile([P, T], F32, name="ra", tag="ra", bufs=1)
+            nc.scalar.activation(ra[:], a_sb[r][:], RELU)
+            return ra
+
+        def plane(r):
+            ra = relu(r)
+            nc.gpsimd.tensor_tensor(da[:, :, r], dh[r][:], ra[:], MULT)
+
+        product(0)
+        product(1)
+        turn(0, 0, (0, 1))
+        scatter(0, 0, 0, 256)
+        product(2)
+        product(3)
+        turn(0, 0, (2, 3))
+        scatter(0, 0, 256, 512)
+        turn(1, 0, (0, 1, 2, 3))
+        scatter(1, 0, 0, C)
+        for j in range(4, 8):
+            product(j)
+        turn(0, 1, (0, 1, 2, 3))
+        scatter(0, 1, 0, C)
+        turn(1, 1, (0, 1, 2, 3))
+        scatter(1, 1, 0, C)
+        plane(0)
+        for r in (2, 3):
+            for e in range(E):
+                turn(r, e, (0, 1, 2, 3))
+                scatter(r, e, 0, C)
+            plane(r - 1)
+
+        w1_bf = keep.tile([P, K, PACK], BF16, name="w1_bf", align_bytes=64)
+        w1_w = keep.tile([P, K], U32, name="w1_w", align_bytes=64)
+        w1_s = keep.tile([P, K], U8, name="w1_s", align_bytes=64)
+        nc.scalar.copy(w1_bf[:], w1_raw[:].rearrange("p r k -> p k r"))
+        nc.vector.quantize_mx(out=w1_w[:].bitcast(E4M3), scales=w1_s[:], in_=w1_bf[:].rearrange("p k r -> p (k r)"))
+
+        ra3 = relu(3)
+        da_w = keep.tile([P, T], U32, name="da_w", align_bytes=64)
+        da_s = keep.tile([P, T], U8, name="da_s", align_bytes=64)
+        for h in range(2):
+            cols = slice(h * HALF, (h + 1) * HALF)
+            nc.vector.tensor_tensor(da[:, cols, 3], dh[3][:, cols], ra3[:, cols], MULT)
+        for h in range(2):
+            cols = slice(h * HALF, (h + 1) * HALF)
+            nc.vector.quantize_mx(
+                out=da_w[:, cols].bitcast(E5M2), scales=da_s[:, cols], in_=da[:, cols, :].rearrange("p t r -> p (t r)")
+            )
+        for h in range(2):
+            cols = slice(h * HALF, (h + 1) * HALF)
+            for kt in range(2):
+                acc = psum.tile([P, HALF], F32, name="acc", tag="acc", bufs=4)
+                nc.tensor.matmul_mx(
+                    out=acc[:],
+                    lhsT=w1_w[:, kt * P : (kt + 1) * P].bitcast(E4M3),
+                    lhsT_scale=w1_s[:, kt * P : (kt + 1) * P],
+                    rhs=da_w[:, cols].bitcast(E5M2),
+                    rhs_scale=da_s[:, cols],
+                    start=True,
+                    stop=True,
+                )
+                res = keep.tile([P, HALF], F32, name="res%d_%d" % (h, kt))
+                if kt == 0 or h == 0:
+                    nc.scalar.copy(res[:], acc[:])
+                else:
+                    nc.vector.tensor_copy(res[:], acc[:])
+                nc.sync.dma_start(out[kt * P : (kt + 1) * P, cols], res[:])

@@ -16,12 +16,22 @@ E4M3 = mybir.dt.float8_e4m3fn_x4
 E5M2 = mybir.dt.float8_e5m2_x4
 E2M1 = mybir.dt.float4_e2m1fn_x4
 MULT = mybir.AluOpType.mult
+ADD = mybir.AluOpType.add
+MIN = mybir.AluOpType.min
+MAX = mybir.AluOpType.max
 COPY = mybir.ActivationFunctionType.Copy
 RELU = mybir.ActivationFunctionType.Relu
+F32_MAX = 3.4028234663852886e38
 
 P = 128
 PACK = 4
+LAST = PACK - 1
+PER_COLUMN = 16
+QUADRANTS = 4
+BLOCKS = C // P
 HALF = 512
+SUM_BANKS = 4
+TURN_BANKS = 3
 
 
 def tile_moe_sub_relu2_kernel(
@@ -32,147 +42,182 @@ def tile_moe_sub_relu2_kernel(
         keep = ctx.enter_context(tc.tile_pool(name="keep", bufs=1))
         psum = ctx.enter_context(tc.psum_pool(name="psum", bufs=1))
 
-        offsets = keep.tile([P, T // 16], U16, name="offsets")
+        offsets = keep.tile([P, T // PER_COLUMN], U16, name="offsets")
         dy_w = keep.tile([P, T], I32, name="dy_w", align_bytes=64)
-        dy_s = keep.tile([P, T // 4], I32, name="dy_s", align_bytes=64)
+        dy_s = keep.tile([P, T // 4], I32, name="dy_s", tag="scales_then_w1", align_bytes=64)
         w2_w = keep.tile([P, E, 2 * H], U8, name="w2_w", align_bytes=64)
         w2_s = keep.tile([P, E, H // 4], I32, name="w2_s", align_bytes=64)
-        gate_rows = keep.tile([P, P], F32, name="gate_rows")
+        gate_rows = keep.tile([P, P], F32, name="gate_rows", tag="gate_then_a")
         ident = keep.tile([P, P], F32, name="ident")
 
-        nc.vector.memset(dy_s[:], 0)
+        nc.gpsimd.memset(dy_s[:], 0)
         nc.vector.memset(w2_s[:], 0)
         make_identity(nc, ident[:])
 
         nc.sync.dma_start(offsets[:], offs)
+        nc.sync.dma_start(gate_rows[:], gate[0 : P * P // T, :].rearrange("r (b c) -> (r b) c", c=P))
+        dy_scale_rows = dy_scales[0].bitcast(I32)
+        for q in range(QUADRANTS):
+            nc.sync.dma_start(dy_s[32 * q : 32 * q + 4, :], dy_scale_rows[4 * q : 4 * q + 4, :])
         nc.sync.dma_start(dy_w[:], dy_words[0].rearrange("p t d -> p (t d)").bitcast(I32))
-        dys32 = dy_scales[0].bitcast(I32)
-        for q in range(4):
-            nc.sync.dma_start(dy_s[32 * q : 32 * q + 4, :], dys32[4 * q : 4 * q + 4, :])
-        nc.sync.dma_start(gate_rows[:], gate[0:16, :].rearrange("r (b c) -> (r b) c", c=P))
         nc.sync.dma_start(w2_w[:].bitcast(I32), w2t_words[:, 0].rearrange("e p b -> p e b").bitcast(I32))
-        w2s32 = w2t_scales[:, 0].rearrange("e b i -> b e i").bitcast(I32)
-        for q in range(4):
-            nc.sync.dma_start(w2_s[32 * q : 32 * q + 4, :, :], w2s32[4 * q : 4 * q + 4, :, :])
-        a_rows = a.rearrange("(p r) t -> p r t", r=PACK)
-        a_sb = []
-        for r in range(PACK):
-            a_r = keep.tile([P, T], F32, name="a%d" % r)
-            a_sb.append(a_r)
-        w1_raw = keep.tile([P, PACK, K], F32, name="w1_raw")
-        for r in (1, 2, 3, 0):
-            nc.sync.dma_start(a_sb[r][:], a_rows[:, r, :])
-        nc.sync.dma_start(w1_raw[:], w1t.rearrange("(p r) k -> p r k", r=PACK))
+        w2_scale_rows = w2t_scales[:, 0].rearrange("e b i -> b e i").bitcast(I32)
+        for q in range(QUADRANTS):
+            nc.sync.dma_start(w2_s[32 * q : 32 * q + 4, :, :], w2_scale_rows[4 * q : 4 * q + 4, :, :])
 
-        g_w = keep.tile([P, T], U32, name="g_w", align_bytes=64)
-        g_s = keep.tile([P, T], U8, name="g_s", align_bytes=64)
-        for lo, hi in ((0, 256), (256, 512), (512, 1024)):
-            cols = offsets[:, lo // 16 : hi // 16]
-            nc.vector.tensor_copy(g_w[:, lo:hi], dy_w[:].bitcast(U32).indirect(cols))
-            nc.vector.tensor_copy(g_s[:, lo:hi], dy_s[:].bitcast(U8).indirect(cols))
+        g_w_first = keep.tile([P, P], U32, name="g_w_first", tag="first_words", align_bytes=64)
+        g_w = keep.tile([P, T - P], U32, name="g_w", align_bytes=64)
+        g_s = [keep.tile([P, C], U8, name="g_s0", align_bytes=64)]
+
+        def slot_offsets(lo, hi):
+            return offsets[:, lo // PER_COLUMN : hi // PER_COLUMN]
+
+        def words_of(lo, hi):
+            return g_w_first[:] if lo == 0 else g_w[:, lo - P : hi - P]
+
+        def gather_words(lo, hi):
+            nc.vector.tensor_copy(words_of(lo, hi), dy_w[:].bitcast(U32).indirect(slot_offsets(lo, hi)))
+
+        def gather_scales(e):
+            nc.vector.tensor_copy(g_s[e][:], dy_s[:].bitcast(U8).indirect(slot_offsets(e * C, (e + 1) * C)))
+
+        gather_scales(0)
+        for lo, hi in ((0, P), (P, 2 * P), (2 * P, C), (C, T)):
+            gather_words(lo, hi)
 
         gate_ps = psum.tile([P, P], F32, name="gate_ps")
         nc.tensor.transpose(gate_ps[:], gate_rows[:], ident[:])
-        gate2 = keep.tile([P, 8], F32, name="gate2")
-        nc.scalar.activation(gate2[:], gate_ps[:, 0:8], COPY, scale=2.0)
+        gate2 = keep.tile([P, E * BLOCKS], F32, name="gate2")
+        nc.scalar.activation(gate2[:], gate_ps[:, 0 : E * BLOCKS], COPY, scale=2.0)
 
-        y_t = [keep.tile([P, PACK, P], F32, name="y_t%d" % j) for j in range(8)]
-        y_s = [[keep.tile([P, C], F32, name="y_s%d_%d" % (r, e)) for e in range(E)] for r in range(PACK)]
-        dh = [keep.tile([P, T], F32, name="dh%d" % r) for r in range(PACK)]
+        a_sb = keep.tile([P, PACK, T], F32, name="a_sb", tag="gate_then_a")
+        nc.sync.dma_start(a_sb[:], a.rearrange("(p r) t -> p r t", r=PACK))
+
+        y_t = [keep.tile([P, PACK, P], F32, name="y_t%d" % j) for j in range(E * BLOCKS)]
+        y_s = [keep.tile([P, T], F32, name="y_s%d" % r) for r in range(PACK)]
+        dh = [keep.tile([P, 2 * T if r == LAST else T], F32, name="dh%d" % r) for r in range(PACK)]
         da = keep.tile([P, T, PACK], BF16, name="da", align_bytes=64)
 
         def product(j):
-            e = j // 4
-            acc = psum.tile([P, H], F32, name="acc", tag="acc", bufs=4)
+            e, b = divmod(j, BLOCKS)
+            acc = psum.tile([P, H], F32, name="acc", tag="acc", bufs=SUM_BANKS)
             nc.tensor.matmul_mx(
                 out=acc[:],
-                lhsT=g_w[:, j * P : (j + 1) * P].bitcast(E5M2),
-                lhsT_scale=g_s[:, j * P : (j + 1) * P],
+                lhsT=words_of(j * P, (j + 1) * P).bitcast(E5M2),
+                lhsT_scale=g_s[e][:, b * P : (b + 1) * P],
                 rhs=w2_w[:, e, :].bitcast(E2M1),
                 rhs_scale=w2_s[:, e, :].bitcast(U8),
                 start=True,
                 stop=True,
             )
+            return acc
+
+        def weigh(j, acc, r_lo, r_hi):
             nc.scalar.activation(
-                y_t[j][:], acc[:].rearrange("p (m r) -> p r m", r=PACK), COPY, scale=gate2[:, j : j + 1]
+                y_t[j][:, r_lo:r_hi, :],
+                acc[:].rearrange("p (m r) -> p r m", r=PACK)[:, r_lo:r_hi, :],
+                COPY,
+                scale=gate2[:, j : j + 1],
             )
 
-        def turn(r, e, blocks):
-            bank = psum.tile([P, C], F32, name="bank", tag="bank", bufs=3)
-            for b in blocks:
-                nc.tensor.transpose(bank[:, b * P : (b + 1) * P], y_t[4 * e + b][:, r, :], ident[:])
-            lo, hi = blocks[0] * P, (blocks[-1] + 1) * P
-            nc.scalar.copy(y_s[r][e][:, lo:hi], bank[:, lo:hi])
+        def turn(r, e, b_lo, b_hi):
+            bank = psum.tile([P, C], F32, name="bank", tag="bank", bufs=TURN_BANKS)
+            for b in range(b_lo, b_hi):
+                nc.tensor.transpose(bank[:, b * P : (b + 1) * P], y_t[BLOCKS * e + b][:, r, :], ident[:])
+            nc.scalar.copy(y_s[r][:, e * C + b_lo * P : e * C + b_hi * P], bank[:, b_lo * P : b_hi * P])
 
-        def scatter(r, e, lo, hi):
-            cols = offsets[:, (e * C + lo) // 16 : (e * C + hi) // 16]
-            nc.vector.tensor_copy(dh[r][:].indirect(cols), y_s[r][e][:, lo:hi])
+        def scatter(r, lo, hi):
+            nc.vector.tensor_copy(dh[r][:].indirect(slot_offsets(lo, hi)), y_s[r][:, lo:hi])
 
-        def relu(r):
-            ra = keep.tile([P, T], F32, name="ra", tag="ra", bufs=1)
-            nc.scalar.activation(ra[:], a_sb[r][:], RELU)
-            return ra
+        accs = [product(0)]
+        g_s.append(keep.tile([P, C], U8, name="g_s1", tag="first_words", align_bytes=64))
+        gather_scales(1)
+        w1_raw = keep.tile([P, PACK, K], F32, name="w1_raw", tag="scales_then_w1", align_bytes=64)
+        nc.sync.dma_start(w1_raw[:], w1t.rearrange("(p r) k -> p r k", r=PACK))
 
-        def plane(r):
-            ra = relu(r)
-            nc.gpsimd.tensor_tensor(da[:, :, r], dh[r][:], ra[:], MULT)
+        for b_lo, b_hi in ((0, 1), (1, BLOCKS)):
+            for j in range(b_lo, b_hi):
+                if j > 0:
+                    accs.append(product(j))
+                weigh(j, accs[j], 0, 2)
+            for r in range(2):
+                turn(r, 0, b_lo, b_hi)
+                scatter(r, b_lo * P, b_hi * P)
+        for j in range(BLOCKS):
+            weigh(j, accs[j], 2, PACK)
+        turn(2, 0, 0, BLOCKS)
+        scatter(2, 0, C)
+        for j in range(BLOCKS, E * BLOCKS):
+            weigh(j, product(j), 0, PACK)
 
-        product(0)
-        product(1)
-        turn(0, 0, (0, 1))
-        scatter(0, 0, 0, 256)
-        product(2)
-        product(3)
-        turn(0, 0, (2, 3))
-        scatter(0, 0, 256, 512)
-        turn(1, 0, (0, 1, 2, 3))
-        scatter(1, 0, 0, C)
-        for j in range(4, 8):
-            product(j)
-        turn(0, 1, (0, 1, 2, 3))
-        scatter(0, 1, 0, C)
-        turn(1, 1, (0, 1, 2, 3))
-        scatter(1, 1, 0, C)
-        plane(0)
-        for r in (2, 3):
-            for e in range(E):
-                turn(r, e, (0, 1, 2, 3))
-                scatter(r, e, 0, C)
-            plane(r - 1)
-
+        relu_a = []
+        for r in range(LAST):
+            relu_a.append(keep.tile([P, T], F32, name="ra%d" % r, tag="ra%d" % r))
+            nc.gpsimd.tensor_scalar(relu_a[r][:], a_sb[:, r, :], F32_MAX, 0.0, MIN, MAX)
         w1_bf = keep.tile([P, K, PACK], BF16, name="w1_bf", align_bytes=64)
-        w1_w = keep.tile([P, K], U32, name="w1_w", align_bytes=64)
-        w1_s = keep.tile([P, K], U8, name="w1_s", align_bytes=64)
-        nc.scalar.copy(w1_bf[:], w1_raw[:].rearrange("p r k -> p k r"))
-        nc.vector.quantize_mx(out=w1_w[:].bitcast(E4M3), scales=w1_s[:], in_=w1_bf[:].rearrange("p k r -> p (k r)"))
+        nc.gpsimd.tensor_scalar(w1_bf[:], w1_raw[:].rearrange("p r k -> p k r"), 1.0, 0.0, MULT, ADD)
 
-        ra3 = relu(3)
+        for r in range(LAST):
+            turn(r, 1, 0, BLOCKS)
+            scatter(r, C, T)
+            nc.gpsimd.tensor_tensor(da[:, :, r], dh[r][:], relu_a[r][:], MULT)
+        for e in range(E):
+            turn(LAST, e, 0, BLOCKS)
+        scatter(LAST, 0, T)
+
+        relu_last = keep.tile([P, T], F32, name="ra3", tag="ra%d" % (LAST - 1))
+        nc.scalar.activation(relu_last[:], a_sb[:, LAST, :], RELU)
         da_w = keep.tile([P, T], U32, name="da_w", align_bytes=64)
         da_s = keep.tile([P, T], U8, name="da_s", align_bytes=64)
-        for h in range(2):
-            cols = slice(h * HALF, (h + 1) * HALF)
-            nc.vector.tensor_tensor(da[:, cols, 3], dh[3][:, cols], ra3[:, cols], MULT)
-        for h in range(2):
-            cols = slice(h * HALF, (h + 1) * HALF)
+
+        def last_plane_by_scalar(tag, *edges):
+            first, last = edges[0], edges[-1]
+            dense = keep.tile([P, last - first], BF16, name="dense", tag=tag, align_bytes=64)
+            nc.vector.tensor_tensor(dense[:], dh[LAST][:, first:last], relu_last[:, first:last], MULT)
+            for lo, hi in zip(edges, edges[1:]):
+                nc.scalar.copy(da[:, lo:hi, LAST], dense[:, lo - first : hi - first])
+
+        def last_plane_direct(lo, hi):
+            nc.vector.tensor_tensor(da[:, lo:hi, LAST], dh[LAST][:, lo:hi], relu_last[:, lo:hi], MULT)
+
+        def quantize_tokens(lo, hi):
             nc.vector.quantize_mx(
-                out=da_w[:, cols].bitcast(E5M2), scales=da_s[:, cols], in_=da[:, cols, :].rearrange("p t r -> p (t r)")
+                out=da_w[:, lo:hi].bitcast(E5M2),
+                scales=da_s[:, lo:hi],
+                in_=da[:, lo:hi, :].rearrange("p t r -> p (t r)"),
             )
-        for h in range(2):
+
+        last_plane_by_scalar("dense_then_w1", 0, 256)
+        last_plane_direct(256, HALF)
+        last_plane_by_scalar("dense", HALF, 768, 896)
+        w1_w = keep.tile([P, K], U32, name="w1_w", tag="dense_then_w1", align_bytes=64)
+        w1_s = keep.tile([P, K], U8, name="w1_s", align_bytes=64)
+        nc.vector.quantize_mx(out=w1_w[:].bitcast(E4M3), scales=w1_s[:], in_=w1_bf[:].rearrange("p k r -> p (k r)"))
+        quantize_tokens(0, HALF)
+        last_plane_direct(896, T)
+        quantize_tokens(HALF, 768)
+        quantize_tokens(768, T)
+
+        for h in range(T // HALF):
             cols = slice(h * HALF, (h + 1) * HALF)
-            for kt in range(2):
-                acc = psum.tile([P, HALF], F32, name="acc", tag="acc", bufs=4)
+            for kt in range(K // P):
+                rows = slice(kt * P, (kt + 1) * P)
+                acc = psum.tile([P, HALF], F32, name="acc", tag="acc", bufs=SUM_BANKS)
                 nc.tensor.matmul_mx(
                     out=acc[:],
-                    lhsT=w1_w[:, kt * P : (kt + 1) * P].bitcast(E4M3),
-                    lhsT_scale=w1_s[:, kt * P : (kt + 1) * P],
+                    lhsT=w1_w[:, rows].bitcast(E4M3),
+                    lhsT_scale=w1_s[:, rows],
                     rhs=da_w[:, cols].bitcast(E5M2),
                     rhs_scale=da_s[:, cols],
                     start=True,
                     stop=True,
                 )
                 res = keep.tile([P, HALF], F32, name="res%d_%d" % (h, kt))
-                if kt == 0 or h == 0:
+                if (h, kt) != (T // HALF - 1, K // P - 1):
                     nc.scalar.copy(res[:], acc[:])
+                    nc.sync.dma_start(out[rows, cols], res[:])
                 else:
-                    nc.vector.tensor_copy(res[:], acc[:])
-                nc.sync.dma_start(out[kt * P : (kt + 1) * P, cols], res[:])
+                    for lo in (0, HALF // 2):
+                        hi = lo + HALF // 2
+                        nc.vector.tensor_copy(res[:, lo:hi], acc[:, lo:hi])
+                        nc.sync.dma_start(out[rows, h * HALF + lo : h * HALF + hi], res[:, lo:hi])

@@ -30,6 +30,7 @@ PER_COLUMN = 16
 QUADRANTS = 4
 BLOCKS = C // P
 HALF = 512
+PARTS = ((0, 512), (512, 768), (768, 1024))
 SUM_BANKS = 4
 TURN_BANKS = 3
 
@@ -43,11 +44,11 @@ def tile_moe_sub_relu2_kernel(
         psum = ctx.enter_context(tc.psum_pool(name="psum", bufs=1))
 
         offsets = keep.tile([P, T // PER_COLUMN], U16, name="offsets")
-        dy_w = keep.tile([P, T], I32, name="dy_w", align_bytes=64)
+        dy_w = keep.tile([P, T], I32, name="dy_w", tag="words_then_a", align_bytes=64)
         dy_s = keep.tile([P, T // 4], I32, name="dy_s", tag="scales_then_w1", align_bytes=64)
         w2_w = keep.tile([P, E, 2 * H], U8, name="w2_w", align_bytes=64)
         w2_s = keep.tile([P, E, H // 4], I32, name="w2_s", align_bytes=64)
-        gate_rows = keep.tile([P, P], F32, name="gate_rows", tag="gate_then_a")
+        gate_rows = keep.tile([P, P], F32, name="gate_rows")
         ident = keep.tile([P, P], F32, name="ident")
 
         nc.gpsimd.memset(dy_s[:], 0)
@@ -90,13 +91,20 @@ def tile_moe_sub_relu2_kernel(
         gate2 = keep.tile([P, E * BLOCKS], F32, name="gate2")
         nc.scalar.activation(gate2[:], gate_ps[:, 0 : E * BLOCKS], COPY, scale=2.0)
 
-        a_sb = keep.tile([P, PACK, T], F32, name="a_sb", tag="gate_then_a")
+        a_sb = keep.tile([P, PACK, T], F32, name="a_sb", tag="words_then_a", align_bytes=64)
         nc.sync.dma_start(a_sb[:], a.rearrange("(p r) t -> p r t", r=PACK))
 
         y_t = [keep.tile([P, PACK, P], F32, name="y_t%d" % j) for j in range(E * BLOCKS)]
         y_s = [keep.tile([P, T], F32, name="y_s%d" % r) for r in range(PACK)]
-        dh = [keep.tile([P, 2 * T if r == LAST else T], F32, name="dh%d" % r) for r in range(PACK)]
-        da = keep.tile([P, T, PACK], BF16, name="da", align_bytes=64)
+        dh = [
+            keep.tile([P, 2 * T if r == LAST else T], F32, name="dh%d" % r, tag="dh%d" % r, align_bytes=64)
+            for r in range(PACK)
+        ]
+        da = {lo: keep.tile([P, hi - lo, PACK], BF16, name="da%d" % lo, align_bytes=64) for lo, hi in PARTS}
+
+        def da_plane(r, lo, hi):
+            first = max(f for f in da if f <= lo)
+            return da[first][:, lo - first : hi - first, r]
 
         def product(j):
             e, b = divmod(j, BLOCKS)
@@ -160,7 +168,8 @@ def tile_moe_sub_relu2_kernel(
         for r in range(LAST):
             turn(r, 1, 0, BLOCKS)
             scatter(r, C, T)
-            nc.gpsimd.tensor_tensor(da[:, :, r], dh[r][:], relu_a[r][:], MULT)
+            for lo, hi in PARTS:
+                nc.gpsimd.tensor_tensor(da_plane(r, lo, hi), dh[r][:, lo:hi], relu_a[r][:, lo:hi], MULT)
         for e in range(E):
             turn(LAST, e, 0, BLOCKS)
         scatter(LAST, 0, T)
@@ -170,33 +179,36 @@ def tile_moe_sub_relu2_kernel(
         da_w = keep.tile([P, T], U32, name="da_w", align_bytes=64)
         da_s = keep.tile([P, T], U8, name="da_s", align_bytes=64)
 
-        def last_plane_by_scalar(tag, *edges):
-            first, last = edges[0], edges[-1]
-            dense = keep.tile([P, last - first], BF16, name="dense", tag=tag, align_bytes=64)
-            nc.vector.tensor_tensor(dense[:], dh[LAST][:, first:last], relu_last[:, first:last], MULT)
-            for lo, hi in zip(edges, edges[1:]):
-                nc.scalar.copy(da[:, lo:hi, LAST], dense[:, lo - first : hi - first])
+        def last_plane_dense(lo, hi):
+            dense = keep.tile([P, hi - lo], BF16, name="dense%d" % lo, align_bytes=64)
+            nc.vector.tensor_tensor(dense[:], dh[LAST][:, lo:hi], relu_last[:, lo:hi], MULT)
+            return dense
+
+        def place(dense, lo, hi, first):
+            nc.scalar.copy(da_plane(LAST, lo, hi), dense[:, lo - first : hi - first])
 
         def last_plane_direct(lo, hi):
-            nc.vector.tensor_tensor(da[:, lo:hi, LAST], dh[LAST][:, lo:hi], relu_last[:, lo:hi], MULT)
+            nc.vector.tensor_tensor(da_plane(LAST, lo, hi), dh[LAST][:, lo:hi], relu_last[:, lo:hi], MULT)
 
         def quantize_tokens(lo, hi):
             nc.vector.quantize_mx(
                 out=da_w[:, lo:hi].bitcast(E5M2),
                 scales=da_s[:, lo:hi],
-                in_=da[:, lo:hi, :].rearrange("p t r -> p (t r)"),
+                in_=da[lo][:].rearrange("p t r -> p (t r)"),
             )
 
-        last_plane_by_scalar("dense_then_w1", 0, 256)
-        last_plane_direct(256, HALF)
-        last_plane_by_scalar("dense", HALF, 768, 896)
-        w1_w = keep.tile([P, K], U32, name="w1_w", tag="dense_then_w1", align_bytes=64)
+        w1_w = keep.tile([P, K], U32, name="w1_w", tag="dh%d" % (LAST - 1), align_bytes=64)
         w1_s = keep.tile([P, K], U8, name="w1_s", align_bytes=64)
         nc.vector.quantize_mx(out=w1_w[:].bitcast(E4M3), scales=w1_s[:], in_=w1_bf[:].rearrange("p k r -> p (k r)"))
-        quantize_tokens(0, HALF)
+        place(last_plane_dense(0, 288), 0, 288, 0)
+        last_plane_direct(288, 512)
+        dense_late = last_plane_dense(512, 896)
+        place(dense_late, 512, 768, 512)
+        place(dense_late, 768, 896, 512)
+        quantize_tokens(*PARTS[0])
         last_plane_direct(896, T)
-        quantize_tokens(HALF, 768)
-        quantize_tokens(768, T)
+        quantize_tokens(*PARTS[1])
+        quantize_tokens(*PARTS[2])
 
         for h in range(T // HALF):
             cols = slice(h * HALF, (h + 1) * HALF)

@@ -31,6 +31,7 @@ QUADRANTS = 4
 BLOCKS = C // P
 HALF = 512
 PARTS = ((0, 512), (512, 768), (768, 1024))
+POOL_LO, POOL_HI = 256, 512
 SUM_BANKS = 4
 TURN_BANKS = 3
 
@@ -162,6 +163,8 @@ def tile_moe_sub_relu2_kernel(
         for r in range(LAST):
             relu_a.append(keep.tile([P, T], F32, name="ra%d" % r, tag="ra%d" % r))
             nc.gpsimd.tensor_scalar(relu_a[r][:], a_sb[:, r, :], F32_MAX, 0.0, MIN, MAX)
+        relu_pool = keep.tile([P, POOL_HI - POOL_LO], F32, name="relu_pool")
+        nc.gpsimd.tensor_scalar(relu_pool[:], a_sb[:, LAST, POOL_LO:POOL_HI], F32_MAX, 0.0, MIN, MAX)
         w1_bf = keep.tile([P, K, PACK], BF16, name="w1_bf", align_bytes=64)
         nc.gpsimd.tensor_scalar(w1_bf[:], w1_raw[:].rearrange("p r k -> p k r"), 1.0, 0.0, MULT, ADD)
 
@@ -174,21 +177,35 @@ def tile_moe_sub_relu2_kernel(
             turn(LAST, e, 0, BLOCKS)
         scatter(LAST, 0, T)
 
-        relu_last = keep.tile([P, T], F32, name="ra3", tag="ra%d" % (LAST - 1))
-        nc.scalar.activation(relu_last[:], a_sb[:, LAST, :], RELU)
+        a_turned = keep.tile([P, T], F32, name="a_turned", tag="ra%d" % (LAST - 1))
+        relu_last = {}
+        for lo, hi in ((0, POOL_LO), (POOL_HI, T)):
+            there = psum.tile([P, HALF], F32, name="acc", tag="acc", bufs=SUM_BANKS)
+            back = psum.tile([P, C], F32, name="bank", tag="bank", bufs=TURN_BANKS)
+            for t in range(lo, hi, P):
+                nc.tensor.transpose(there[:, t - lo : t - lo + P], a_sb[:, LAST, t : t + P], ident[:])
+            nc.scalar.activation(a_turned[:, lo:hi], there[:, 0 : hi - lo], RELU)
+            for t in range(lo, hi, P):
+                nc.tensor.transpose(back[:, t - lo : t - lo + P], a_turned[:, t : t + P], ident[:])
+            relu_last[lo] = back
+
+        def relu_in_psum(lo, hi):
+            first = max(f for f in relu_last if f <= lo)
+            return relu_last[first][:, lo - first : hi - first]
+
         da_w = keep.tile([P, T], U32, name="da_w", align_bytes=64)
         da_s = keep.tile([P, T], U8, name="da_s", align_bytes=64)
 
         def last_plane_dense(lo, hi):
             dense = keep.tile([P, hi - lo], BF16, name="dense%d" % lo, align_bytes=64)
-            nc.vector.tensor_tensor(dense[:], dh[LAST][:, lo:hi], relu_last[:, lo:hi], MULT)
+            nc.vector.tensor_tensor(dense[:], dh[LAST][:, lo:hi], relu_in_psum(lo, hi), MULT)
             return dense
 
         def place(dense, lo, hi, first):
             nc.scalar.copy(da_plane(LAST, lo, hi), dense[:, lo - first : hi - first])
 
         def last_plane_direct(lo, hi):
-            nc.vector.tensor_tensor(da_plane(LAST, lo, hi), dh[LAST][:, lo:hi], relu_last[:, lo:hi], MULT)
+            nc.vector.tensor_tensor(da_plane(LAST, lo, hi), dh[LAST][:, lo:hi], relu_in_psum(lo, hi), MULT)
 
         def quantize_tokens(lo, hi):
             nc.vector.quantize_mx(
@@ -200,8 +217,11 @@ def tile_moe_sub_relu2_kernel(
         w1_w = keep.tile([P, K], U32, name="w1_w", tag="dh%d" % (LAST - 1), align_bytes=64)
         w1_s = keep.tile([P, K], U8, name="w1_s", align_bytes=64)
         nc.vector.quantize_mx(out=w1_w[:].bitcast(E4M3), scales=w1_s[:], in_=w1_bf[:].rearrange("p k r -> p (k r)"))
-        place(last_plane_dense(0, 288), 0, 288, 0)
-        last_plane_direct(288, 512)
+        nc.gpsimd.tensor_tensor(
+            da_plane(LAST, POOL_LO, POOL_HI), dh[LAST][:, POOL_LO:POOL_HI], relu_pool[:], MULT
+        )
+        place(last_plane_dense(0, 176), 0, 176, 0)
+        last_plane_direct(176, POOL_LO)
         dense_late = last_plane_dense(512, 896)
         place(dense_late, 512, 768, 512)
         place(dense_late, 768, 896, 512)

@@ -98,14 +98,13 @@ def tile_moe_sub_relu2_kernel(
         y_t = [keep.tile([P, PACK, P], F32, name="y_t%d" % j) for j in range(E * BLOCKS)]
         y_s = [keep.tile([P, T], F32, name="y_s%d" % r) for r in range(PACK)]
         dh = [
-            keep.tile([P, 2 * T if r == LAST else T], F32, name="dh%d" % r, tag="dh%d" % r, align_bytes=64)
+            keep.tile([P, 2 * T if r >= 2 else T], F32, name="dh%d" % r, tag="dh%d" % r, align_bytes=64)
             for r in range(PACK)
         ]
-        da = {lo: keep.tile([P, hi - lo, PACK], BF16, name="da%d" % lo, align_bytes=64) for lo, hi in PARTS}
+        da = keep.tile([P, T, PACK], BF16, name="da", align_bytes=64)
 
         def da_plane(r, lo, hi):
-            first = max(f for f in da if f <= lo)
-            return da[first][:, lo - first : hi - first, r]
+            return da[:, lo:hi, r]
 
         def product(j):
             e, b = divmod(j, BLOCKS)
@@ -154,10 +153,9 @@ def tile_moe_sub_relu2_kernel(
                 scatter(r, b_lo * P, b_hi * P)
         for j in range(BLOCKS):
             weigh(j, accs[j], 2, PACK)
-        turn(2, 0, 0, BLOCKS)
-        scatter(2, 0, C)
         for j in range(BLOCKS, E * BLOCKS):
-            weigh(j, product(j), 0, PACK)
+            accs.append(product(j))
+            weigh(j, accs[j], 0, 2)
 
         relu_a = []
         for r in range(LAST):
@@ -168,14 +166,21 @@ def tile_moe_sub_relu2_kernel(
         w1_bf = keep.tile([P, K, PACK], BF16, name="w1_bf", align_bytes=64)
         nc.gpsimd.tensor_scalar(w1_bf[:], w1_raw[:].rearrange("p r k -> p k r"), 1.0, 0.0, MULT, ADD)
 
-        for r in range(LAST):
+        def multiply(r):
+            nc.gpsimd.tensor_tensor(da_plane(r, 0, T), dh[r][:, 0:T], relu_a[r][:], MULT)
+
+        for r in range(2):
             turn(r, 1, 0, BLOCKS)
             scatter(r, C, T)
-            for lo, hi in PARTS:
-                nc.gpsimd.tensor_tensor(da_plane(r, lo, hi), dh[r][:, lo:hi], relu_a[r][:, lo:hi], MULT)
-        for e in range(E):
-            turn(LAST, e, 0, BLOCKS)
-        scatter(LAST, 0, T)
+            multiply(r)
+        for j in range(BLOCKS, E * BLOCKS):
+            weigh(j, accs[j], 2, PACK)
+        for r in range(2, PACK):
+            for e in range(E):
+                turn(r, e, 0, BLOCKS)
+            scatter(r, 0, T)
+            if r < LAST:
+                multiply(r)
 
         a_turned = keep.tile([P, T], F32, name="a_turned", tag="ra%d" % (LAST - 1))
         relu_last = {}
@@ -211,7 +216,7 @@ def tile_moe_sub_relu2_kernel(
             nc.vector.quantize_mx(
                 out=da_w[:, lo:hi].bitcast(E5M2),
                 scales=da_s[:, lo:hi],
-                in_=da[lo][:].rearrange("p t r -> p (t r)"),
+                in_=da[:, lo:hi, :].rearrange("p t r -> p (t r)"),
             )
 
         w1_w = keep.tile([P, K], U32, name="w1_w", tag="dh%d" % (LAST - 1), align_bytes=64)
@@ -245,11 +250,8 @@ def tile_moe_sub_relu2_kernel(
                     stop=True,
                 )
                 res = keep.tile([P, HALF], F32, name="res%d_%d" % (h, kt))
-                if (h, kt) != (T // HALF - 1, K // P - 1):
-                    nc.scalar.copy(res[:], acc[:])
-                    nc.sync.dma_start(out[rows, cols], res[:])
-                else:
-                    for lo in (0, HALF // 2):
-                        hi = lo + HALF // 2
-                        nc.vector.tensor_copy(res[:, lo:hi], acc[:, lo:hi])
-                        nc.sync.dma_start(out[rows, h * HALF + lo : h * HALF + hi], res[:, lo:hi])
+                copy = nc.vector.tensor_copy if (h, kt) == (1, 0) else nc.scalar.copy
+                edges = {(0, 0): (0, 128, HALF), (1, 1): (0, 320, HALF)}.get((h, kt), (0, HALF))
+                for lo, hi in zip(edges, edges[1:]):
+                    copy(res[:, lo:hi], acc[:, lo:hi])
+                    nc.sync.dma_start(out[rows, h * HALF + lo : h * HALF + hi], res[:, lo:hi])

@@ -32,8 +32,9 @@ BLOCKS = C // P
 HALF = 512
 PARTS = ((0, 512), (512, 768), (768, 1024))
 POOL_LO, POOL_HI = 256, 512
-SUM_BANKS = 4
-TURN_BANKS = 3
+HELD_BLOCK = 2
+SUM_BANKS = 3
+TURN_BANKS = 4
 
 
 def tile_moe_sub_relu2_kernel(
@@ -47,7 +48,7 @@ def tile_moe_sub_relu2_kernel(
         offsets = keep.tile([P, T // PER_COLUMN], U16, name="offsets")
         dy_w = keep.tile([P, T], I32, name="dy_w", tag="words_then_a", align_bytes=64)
         dy_s = keep.tile([P, T // 4], I32, name="dy_s", tag="scales_then_w1", align_bytes=64)
-        w2_w = keep.tile([P, E, 2 * H], U8, name="w2_w", align_bytes=64)
+        w2_w = [keep.tile([P, 2 * H], U8, name="w2_w%d" % e, align_bytes=64) for e in range(E)]
         w2_s = keep.tile([P, E, H // 4], I32, name="w2_s", align_bytes=64)
         gate_rows = keep.tile([P, P], F32, name="gate_rows")
         ident = keep.tile([P, P], F32, name="ident")
@@ -58,14 +59,15 @@ def tile_moe_sub_relu2_kernel(
 
         nc.sync.dma_start(offsets[:], offs)
         nc.sync.dma_start(gate_rows[:], gate[0 : P * P // T, :].rearrange("r (b c) -> (r b) c", c=P))
+        nc.sync.dma_start(w2_w[0][:].bitcast(I32), w2t_words[0, 0].bitcast(I32))
         dy_scale_rows = dy_scales[0].bitcast(I32)
         for q in range(QUADRANTS):
             nc.sync.dma_start(dy_s[32 * q : 32 * q + 4, :], dy_scale_rows[4 * q : 4 * q + 4, :])
         nc.sync.dma_start(dy_w[:], dy_words[0].rearrange("p t d -> p (t d)").bitcast(I32))
-        nc.sync.dma_start(w2_w[:].bitcast(I32), w2t_words[:, 0].rearrange("e p b -> p e b").bitcast(I32))
         w2_scale_rows = w2t_scales[:, 0].rearrange("e b i -> b e i").bitcast(I32)
         for q in range(QUADRANTS):
             nc.sync.dma_start(w2_s[32 * q : 32 * q + 4, :, :], w2_scale_rows[4 * q : 4 * q + 4, :, :])
+        nc.sync.dma_start(w2_w[1][:].bitcast(I32), w2t_words[1, 0].bitcast(I32))
 
         g_w_first = keep.tile([P, P], U32, name="g_w_first", tag="first_words", align_bytes=64)
         g_w = keep.tile([P, T - P], U32, name="g_w", align_bytes=64)
@@ -87,7 +89,7 @@ def tile_moe_sub_relu2_kernel(
         for lo, hi in ((0, P), (P, 2 * P), (2 * P, C), (C, T)):
             gather_words(lo, hi)
 
-        gate_ps = psum.tile([P, P], F32, name="gate_ps")
+        gate_ps = psum.tile([P, P], F32, name="gate_ps", tag="spare")
         nc.tensor.transpose(gate_ps[:], gate_rows[:], ident[:])
         gate2 = keep.tile([P, E * BLOCKS], F32, name="gate2")
         nc.scalar.activation(gate2[:], gate_ps[:, 0 : E * BLOCKS], COPY, scale=2.0)
@@ -106,14 +108,19 @@ def tile_moe_sub_relu2_kernel(
         def da_plane(r, lo, hi):
             return da[:, lo:hi, r]
 
+        def sum_bank(b):
+            if b == HELD_BLOCK:
+                return psum.tile([P, H], F32, name="held", tag="spare")
+            return psum.tile([P, H], F32, name="acc", tag="acc", bufs=SUM_BANKS)
+
         def product(j):
             e, b = divmod(j, BLOCKS)
-            acc = psum.tile([P, H], F32, name="acc", tag="acc", bufs=SUM_BANKS)
+            acc = sum_bank(b)
             nc.tensor.matmul_mx(
                 out=acc[:],
                 lhsT=words_of(j * P, (j + 1) * P).bitcast(E5M2),
                 lhsT_scale=g_s[e][:, b * P : (b + 1) * P],
-                rhs=w2_w[:, e, :].bitcast(E2M1),
+                rhs=w2_w[e][:].bitcast(E2M1),
                 rhs_scale=w2_s[:, e, :].bitcast(U8),
                 start=True,
                 stop=True,
@@ -129,7 +136,10 @@ def tile_moe_sub_relu2_kernel(
             )
 
         def turn(r, e, b_lo, b_hi):
-            bank = psum.tile([P, C], F32, name="bank", tag="bank", bufs=TURN_BANKS)
+            if (r, e, b_lo) == (0, 0, 0) and b_hi == 1:
+                bank = psum.tile([P, C], F32, name="bank", tag="spare")
+            else:
+                bank = psum.tile([P, C], F32, name="bank", tag="bank", bufs=TURN_BANKS)
             for b in range(b_lo, b_hi):
                 nc.tensor.transpose(bank[:, b * P : (b + 1) * P], y_t[BLOCKS * e + b][:, r, :], ident[:])
             nc.scalar.copy(y_s[r][:, e * C + b_lo * P : e * C + b_hi * P], bank[:, b_lo * P : b_hi * P])
@@ -143,10 +153,13 @@ def tile_moe_sub_relu2_kernel(
         w1_raw = keep.tile([P, PACK, K], F32, name="w1_raw", tag="scales_then_w1", align_bytes=64)
         nc.sync.dma_start(w1_raw[:], w1t.rearrange("(p r) k -> p r k", r=PACK))
 
-        for b_lo, b_hi in ((0, 1), (1, BLOCKS)):
+        for r in range(2):
+            weigh(0, accs[0], r, r + 1)
+            turn(r, 0, 0, 1)
+            scatter(r, 0, P)
+        for b_lo, b_hi in ((1, 2), (2, BLOCKS)):
             for j in range(b_lo, b_hi):
-                if j > 0:
-                    accs.append(product(j))
+                accs.append(product(j))
                 weigh(j, accs[j], 0, 2)
             for r in range(2):
                 turn(r, 0, b_lo, b_hi)
@@ -239,7 +252,7 @@ def tile_moe_sub_relu2_kernel(
             cols = slice(h * HALF, (h + 1) * HALF)
             for kt in range(K // P):
                 rows = slice(kt * P, (kt + 1) * P)
-                acc = psum.tile([P, HALF], F32, name="acc", tag="acc", bufs=SUM_BANKS)
+                acc = sum_bank(h * (K // P) + kt)
                 nc.tensor.matmul_mx(
                     out=acc[:],
                     lhsT=w1_w[:, rows].bitcast(E4M3),

@@ -263,8 +263,8 @@ def tile_moe_sub_relu2_kernel(
                     stop=True,
                 )
                 res = keep.tile([P, HALF], F32, name="res%d_%d" % (h, kt))
-                copy = nc.vector.tensor_copy if (h, kt) == (1, 0) else nc.scalar.copy
-                edges = {(0, 0): (0, 128, HALF), (1, 1): (0, 320, HALF)}.get((h, kt), (0, HALF))
-                for lo, hi in zip(edges, edges[1:]):
+                copy = nc.scalar.copy if kt == 0 else nc.vector.tensor_copy
+                for lo in (0, HALF // 2):
+                    hi = lo + HALF // 2
                     copy(res[:, lo:hi], acc[:, lo:hi])
                     nc.sync.dma_start(out[rows, h * HALF + lo : h * HALF + hi], res[:, lo:hi])

@@ -53,17 +53,16 @@ def tile_moe_sub_relu2_kernel(
         gate_rows = keep.tile([P, P], F32, name="gate_rows")
         ident = keep.tile([P, P], F32, name="ident")
 
-        nc.gpsimd.memset(dy_s[:], 0)
         nc.vector.memset(w2_s[:], 0)
         make_identity(nc, ident[:])
 
         nc.sync.dma_start(offsets[:], offs)
-        nc.sync.dma_start(gate_rows[:], gate[0 : P * P // T, :].rearrange("r (b c) -> (r b) c", c=P))
-        nc.sync.dma_start(w2_w[0][:].bitcast(I32), w2t_words[0, 0].bitcast(I32))
         dy_scale_rows = dy_scales[0].bitcast(I32)
         for q in range(QUADRANTS):
-            nc.sync.dma_start(dy_s[32 * q : 32 * q + 4, :], dy_scale_rows[4 * q : 4 * q + 4, :])
+            nc.sync.dma_start(dy_s[32 * q : 32 * q + 32, :], dy_scale_rows[4 * q : 4 * q + 4, :].partition_broadcast(8))
         nc.sync.dma_start(dy_w[:], dy_words[0].rearrange("p t d -> p (t d)").bitcast(I32))
+        nc.sync.dma_start(w2_w[0][:].bitcast(I32), w2t_words[0, 0].bitcast(I32))
+        nc.sync.dma_start(gate_rows[:], gate[0 : P * P // T, :].rearrange("r (b c) -> (r b) c", c=P))
         w2_scale_rows = w2t_scales[:, 0].rearrange("e b i -> b e i").bitcast(I32)
         for q in range(QUADRANTS):
             nc.sync.dma_start(w2_s[32 * q : 32 * q + 4, :, :], w2_scale_rows[4 * q : 4 * q + 4, :, :])

@@ -32,6 +32,7 @@ BLOCKS = C // P
 HALF = 512
 PARTS = ((0, 512), (512, 768), (768, 1024))
 POOL_LO, POOL_HI = 256, 512
+ALIGN = 256
 HELD_BLOCK = 2
 SUM_BANKS = 3
 TURN_BANKS = 4
@@ -45,13 +46,13 @@ def tile_moe_sub_relu2_kernel(
         keep = ctx.enter_context(tc.tile_pool(name="keep", bufs=1))
         psum = ctx.enter_context(tc.psum_pool(name="psum", bufs=1))
 
-        offsets = keep.tile([P, T // PER_COLUMN], U16, name="offsets")
-        dy_w = keep.tile([P, T], I32, name="dy_w", tag="words_then_a", align_bytes=64)
-        dy_s = keep.tile([P, T // 4], I32, name="dy_s", tag="scales_then_w1", align_bytes=64)
-        w2_w = [keep.tile([P, 2 * H], U8, name="w2_w%d" % e, align_bytes=64) for e in range(E)]
-        w2_s = keep.tile([P, E, H // 4], I32, name="w2_s", align_bytes=64)
-        gate_rows = keep.tile([P, P], F32, name="gate_rows")
-        ident = keep.tile([P, P], F32, name="ident")
+        offsets = keep.tile([P, T // PER_COLUMN], U16, name="offsets", align_bytes=ALIGN)
+        dy_w = keep.tile([P, T], I32, name="dy_w", tag="words_then_a", align_bytes=ALIGN)
+        dy_s = keep.tile([P, T // 4], I32, name="dy_s", tag="scales_then_w1", align_bytes=ALIGN)
+        w2_w = [keep.tile([P, 2 * H], U8, name="w2_w%d" % e, align_bytes=ALIGN) for e in range(E)]
+        w2_s = keep.tile([P, E, H // 4], I32, name="w2_s", align_bytes=ALIGN)
+        gate_rows = keep.tile([P, P], F32, name="gate_rows", align_bytes=ALIGN)
+        ident = keep.tile([P, P], F32, name="ident", align_bytes=ALIGN)
 
         nc.vector.memset(w2_s[:], 0)
         make_identity(nc, ident[:])
@@ -68,9 +69,9 @@ def tile_moe_sub_relu2_kernel(
             nc.sync.dma_start(w2_s[32 * q : 32 * q + 4, :, :], w2_scale_rows[4 * q : 4 * q + 4, :, :])
         nc.sync.dma_start(w2_w[1][:].bitcast(I32), w2t_words[1, 0].bitcast(I32))
 
-        g_w_first = keep.tile([P, P], U32, name="g_w_first", tag="first_words", align_bytes=64)
-        g_w = keep.tile([P, T - P], U32, name="g_w", align_bytes=64)
-        g_s = [keep.tile([P, C], U8, name="g_s0", align_bytes=64)]
+        g_w_first = keep.tile([P, P], U32, name="g_w_first", tag="first_words", align_bytes=ALIGN)
+        g_w = keep.tile([P, T - P], U32, name="g_w", align_bytes=ALIGN)
+        g_s = [keep.tile([P, C], U8, name="g_s0", align_bytes=ALIGN)]
 
         def slot_offsets(lo, hi):
             return offsets[:, lo // PER_COLUMN : hi // PER_COLUMN]
@@ -90,19 +91,19 @@ def tile_moe_sub_relu2_kernel(
 
         gate_ps = psum.tile([P, P], F32, name="gate_ps", tag="spare")
         nc.tensor.transpose(gate_ps[:], gate_rows[:], ident[:])
-        gate2 = keep.tile([P, E * BLOCKS], F32, name="gate2")
+        gate2 = keep.tile([P, E * BLOCKS], F32, name="gate2", align_bytes=ALIGN)
         nc.scalar.activation(gate2[:], gate_ps[:, 0 : E * BLOCKS], COPY, scale=2.0)
 
-        a_sb = keep.tile([P, PACK, T], F32, name="a_sb", tag="words_then_a", align_bytes=64)
+        a_sb = keep.tile([P, PACK, T], F32, name="a_sb", tag="words_then_a", align_bytes=ALIGN)
         nc.sync.dma_start(a_sb[:], a.rearrange("(p r) t -> p r t", r=PACK))
 
-        y_t = [keep.tile([P, PACK, P], F32, name="y_t%d" % j) for j in range(E * BLOCKS)]
-        y_s = [keep.tile([P, T], F32, name="y_s%d" % r) for r in range(PACK)]
+        y_t = [keep.tile([P, PACK, P], F32, name="y_t%d" % j, align_bytes=ALIGN) for j in range(E * BLOCKS)]
+        y_s = [keep.tile([P, T], F32, name="y_s%d" % r, align_bytes=ALIGN) for r in range(PACK)]
         dh = [
-            keep.tile([P, 2 * T if r >= 2 else T], F32, name="dh%d" % r, tag="dh%d" % r, align_bytes=64)
+            keep.tile([P, 2 * T if r >= 2 else T], F32, name="dh%d" % r, tag="dh%d" % r, align_bytes=ALIGN)
             for r in range(PACK)
         ]
-        da = keep.tile([P, T, PACK], BF16, name="da", align_bytes=64)
+        da = keep.tile([P, T, PACK], BF16, name="da", align_bytes=ALIGN)
 
         def da_plane(r, lo, hi):
             return da[:, lo:hi, r]
@@ -147,9 +148,9 @@ def tile_moe_sub_relu2_kernel(
             nc.vector.tensor_copy(dh[r][:].indirect(slot_offsets(lo, hi)), y_s[r][:, lo:hi])
 
         accs = [product(0)]
-        g_s.append(keep.tile([P, C], U8, name="g_s1", tag="first_words", align_bytes=64))
+        g_s.append(keep.tile([P, C], U8, name="g_s1", tag="first_words", align_bytes=ALIGN))
         gather_scales(1)
-        w1_raw = keep.tile([P, PACK, K], F32, name="w1_raw", tag="scales_then_w1", align_bytes=64)
+        w1_raw = keep.tile([P, PACK, K], F32, name="w1_raw", tag="scales_then_w1", align_bytes=ALIGN)
         nc.sync.dma_start(w1_raw[:], w1t.rearrange("(p r) k -> p r k", r=PACK))
 
         for r in range(2):
@@ -171,11 +172,11 @@ def tile_moe_sub_relu2_kernel(
 
         relu_a = []
         for r in range(LAST):
-            relu_a.append(keep.tile([P, T], F32, name="ra%d" % r, tag="ra%d" % r))
+            relu_a.append(keep.tile([P, T], F32, name="ra%d" % r, tag="ra%d" % r, align_bytes=ALIGN))
             nc.gpsimd.tensor_scalar(relu_a[r][:], a_sb[:, r, :], F32_MAX, 0.0, MIN, MAX)
-        relu_pool = keep.tile([P, POOL_HI - POOL_LO], F32, name="relu_pool")
+        relu_pool = keep.tile([P, POOL_HI - POOL_LO], F32, name="relu_pool", align_bytes=ALIGN)
         nc.gpsimd.tensor_scalar(relu_pool[:], a_sb[:, LAST, POOL_LO:POOL_HI], F32_MAX, 0.0, MIN, MAX)
-        w1_bf = keep.tile([P, K, PACK], BF16, name="w1_bf", align_bytes=64)
+        w1_bf = keep.tile([P, K, PACK], BF16, name="w1_bf", align_bytes=ALIGN)
         nc.gpsimd.tensor_scalar(w1_bf[:], w1_raw[:].rearrange("p r k -> p k r"), 1.0, 0.0, MULT, ADD)
 
         def multiply(r):
@@ -194,7 +195,7 @@ def tile_moe_sub_relu2_kernel(
             if r < LAST:
                 multiply(r)
 
-        a_turned = keep.tile([P, T], F32, name="a_turned", tag="ra%d" % (LAST - 1))
+        a_turned = keep.tile([P, T], F32, name="a_turned", tag="ra%d" % (LAST - 1), align_bytes=ALIGN)
         relu_last = {}
         for lo, hi in ((0, POOL_LO), (POOL_HI, T)):
             there = psum.tile([P, HALF], F32, name="acc", tag="acc", bufs=SUM_BANKS)
@@ -210,11 +211,11 @@ def tile_moe_sub_relu2_kernel(
             first = max(f for f in relu_last if f <= lo)
             return relu_last[first][:, lo - first : hi - first]
 
-        da_w = keep.tile([P, T], U32, name="da_w", align_bytes=64)
-        da_s = keep.tile([P, T], U8, name="da_s", align_bytes=64)
+        da_w = keep.tile([P, T], U32, name="da_w", align_bytes=ALIGN)
+        da_s = keep.tile([P, T], U8, name="da_s", align_bytes=ALIGN)
 
         def last_plane_dense(lo, hi):
-            dense = keep.tile([P, hi - lo], BF16, name="dense%d" % lo, align_bytes=64)
+            dense = keep.tile([P, hi - lo], BF16, name="dense%d" % lo, align_bytes=ALIGN)
             nc.vector.tensor_tensor(dense[:], dh[LAST][:, lo:hi], relu_in_psum(lo, hi), MULT)
             return dense
 
@@ -231,8 +232,8 @@ def tile_moe_sub_relu2_kernel(
                 in_=da[:, lo:hi, :].rearrange("p t r -> p (t r)"),
             )
 
-        w1_w = keep.tile([P, K], U32, name="w1_w", tag="dh%d" % (LAST - 1), align_bytes=64)
-        w1_s = keep.tile([P, K], U8, name="w1_s", align_bytes=64)
+        w1_w = keep.tile([P, K], U32, name="w1_w", tag="dh%d" % (LAST - 1), align_bytes=ALIGN)
+        w1_s = keep.tile([P, K], U8, name="w1_s", align_bytes=ALIGN)
         nc.vector.quantize_mx(out=w1_w[:].bitcast(E4M3), scales=w1_s[:], in_=w1_bf[:].rearrange("p k r -> p (k r)"))
         nc.gpsimd.tensor_tensor(
             da_plane(LAST, POOL_LO, POOL_HI), dh[LAST][:, POOL_LO:POOL_HI], relu_pool[:], MULT
@@ -261,7 +262,7 @@ def tile_moe_sub_relu2_kernel(
                     start=True,
                     stop=True,
                 )
-                res = keep.tile([P, HALF], F32, name="res%d_%d" % (h, kt))
+                res = keep.tile([P, HALF], F32, name="res%d_%d" % (h, kt), align_bytes=ALIGN)
                 copy = nc.scalar.copy if kt == 0 else nc.vector.tensor_copy
                 for lo in (0, HALF // 2):
                     hi = lo + HALF // 2

@@ -16,26 +16,23 @@ E4M3 = mybir.dt.float8_e4m3fn_x4
 E5M2 = mybir.dt.float8_e5m2_x4
 E2M1 = mybir.dt.float4_e2m1fn_x4
 MULT = mybir.AluOpType.mult
-ADD = mybir.AluOpType.add
-MIN = mybir.AluOpType.min
-MAX = mybir.AluOpType.max
 COPY = mybir.ActivationFunctionType.Copy
 RELU = mybir.ActivationFunctionType.Relu
-F32_MAX = 3.4028234663852886e38
 
 P = 128
 PACK = 4
 LAST = PACK - 1
 PER_COLUMN = 16
 QUADRANTS = 4
-BLOCKS = C // P
+RUN = 8
 HALF = 512
 PARTS = ((0, 512), (512, 768), (768, 1024))
 POOL_LO, POOL_HI = 256, 512
+FIRST_EDGE = 176
+SECOND_EDGE = 896
 ALIGN = 256
-HELD_BLOCK = 2
-SUM_BANKS = 3
-TURN_BANKS = 4
+SUM_BANKS = 4
+RELU_BANKS = 2
 
 
 def tile_moe_sub_relu2_kernel(
@@ -46,160 +43,142 @@ def tile_moe_sub_relu2_kernel(
         keep = ctx.enter_context(tc.tile_pool(name="keep", bufs=1))
         psum = ctx.enter_context(tc.psum_pool(name="psum", bufs=1))
 
-        offsets = keep.tile([P, T // PER_COLUMN], U16, name="offsets", align_bytes=ALIGN)
-        dy_w = keep.tile([P, T], I32, name="dy_w", tag="words_then_a", align_bytes=ALIGN)
-        dy_s = keep.tile([P, T // 4], I32, name="dy_s", tag="scales_then_w1", align_bytes=ALIGN)
-        w2_w = [keep.tile([P, 2 * H], U8, name="w2_w%d" % e, align_bytes=ALIGN) for e in range(E)]
-        w2_s = keep.tile([P, E, H // 4], I32, name="w2_s", align_bytes=ALIGN)
-        gate_rows = keep.tile([P, P], F32, name="gate_rows", align_bytes=ALIGN)
-        ident = keep.tile([P, P], F32, name="ident", align_bytes=ALIGN)
+        def tile(shape, dtype, name, tag=None):
+            return keep.tile(shape, dtype, name=name, tag=tag or name, align_bytes=ALIGN)
 
-        nc.vector.memset(w2_s[:], 0)
-        make_identity(nc, ident[:])
+        offsets = tile([P, T // PER_COLUMN], U16, "offsets")
+        dy_w = tile([P, T], I32, "dy_w", "words_then_a")
+        dy_s = tile([P, T // 4], I32, "dy_s", "scales_then_w1")
+        w2_w_raw = [tile([P, H // 2], I32, "w2_w_raw%d" % e) for e in range(E)]
+        w2_s_raw = tile([P, E, H // 4], I32, "w2_s_raw")
+        gates = [tile([P, C], F32, "gate%d" % e) for e in range(E)]
+        ident = tile([P, P], F32, "ident")
+
+        nc.gpsimd.memset(w2_s_raw[:], 0)
 
         nc.sync.dma_start(offsets[:], offs)
         dy_scale_rows = dy_scales[0].bitcast(I32)
         for q in range(QUADRANTS):
-            nc.sync.dma_start(dy_s[32 * q : 32 * q + 32, :], dy_scale_rows[4 * q : 4 * q + 4, :].partition_broadcast(8))
+            queue = nc.sync if q < 2 else nc.scalar
+            queue.dma_start(dy_s[32 * q : 32 * q + 32, :], dy_scale_rows[4 * q : 4 * q + 4, :].partition_broadcast(8))
         nc.sync.dma_start(dy_w[:], dy_words[0].rearrange("p t d -> p (t d)").bitcast(I32))
-        nc.sync.dma_start(w2_w[0][:].bitcast(I32), w2t_words[0, 0].bitcast(I32))
-        nc.sync.dma_start(gate_rows[:], gate[0 : P * P // T, :].rearrange("r (b c) -> (r b) c", c=P))
+        nc.sync.dma_start(w2_w_raw[0][:], w2t_words[0, 0].bitcast(I32))
         w2_scale_rows = w2t_scales[:, 0].rearrange("e b i -> b e i").bitcast(I32)
         for q in range(QUADRANTS):
-            nc.sync.dma_start(w2_s[32 * q : 32 * q + 4, :, :], w2_scale_rows[4 * q : 4 * q + 4, :, :])
-        nc.sync.dma_start(w2_w[1][:].bitcast(I32), w2t_words[1, 0].bitcast(I32))
+            nc.sync.dma_start(w2_s_raw[32 * q : 32 * q + 4, :, :], w2_scale_rows[4 * q : 4 * q + 4, :, :])
+        nc.sync.dma_start(gates[0][:], gate[:, 0:C])
+        nc.sync.dma_start(w2_w_raw[1][:], w2t_words[1, 0].bitcast(I32))
+        nc.sync.dma_start(gates[1][:], gate[:, C:T])
+        make_identity(nc, ident[:])
 
-        g_w_first = keep.tile([P, P], U32, name="g_w_first", tag="first_words", align_bytes=ALIGN)
-        g_w = keep.tile([P, T - P], U32, name="g_w", align_bytes=ALIGN)
-        g_s = [keep.tile([P, C], U8, name="g_s0", align_bytes=ALIGN)]
+        g_w = [tile([P, C], U32, "g_w%d" % e) for e in range(E)]
+        g_s = [tile([P, C], U8, "g_s0")]
 
         def slot_offsets(lo, hi):
             return offsets[:, lo // PER_COLUMN : hi // PER_COLUMN]
-
-        def words_of(lo, hi):
-            return g_w_first[:] if lo == 0 else g_w[:, lo - P : hi - P]
-
-        def gather_words(lo, hi):
-            nc.vector.tensor_copy(words_of(lo, hi), dy_w[:].bitcast(U32).indirect(slot_offsets(lo, hi)))
 
         def gather_scales(e):
             nc.vector.tensor_copy(g_s[e][:], dy_s[:].bitcast(U8).indirect(slot_offsets(e * C, (e + 1) * C)))
 
         gather_scales(0)
-        for lo, hi in ((0, P), (P, 2 * P), (2 * P, C), (C, T)):
-            gather_words(lo, hi)
+        for e in range(E):
+            nc.vector.tensor_copy(g_w[e][:], dy_w[:].bitcast(U32).indirect(slot_offsets(e * C, (e + 1) * C)))
 
-        gate_ps = psum.tile([P, P], F32, name="gate_ps", tag="spare")
-        nc.tensor.transpose(gate_ps[:], gate_rows[:], ident[:])
-        gate2 = keep.tile([P, E * BLOCKS], F32, name="gate2", align_bytes=ALIGN)
-        nc.scalar.activation(gate2[:], gate_ps[:, 0 : E * BLOCKS], COPY, scale=2.0)
+        w2_w = [tile([P, H // 2], I32, "w2_w%d" % e) for e in range(E)]
+        w2_s = [tile([P, H // 4], I32, "w2_s%d" % e) for e in range(E)]
 
-        a_sb = keep.tile([P, PACK, T], F32, name="a_sb", tag="words_then_a", align_bytes=ALIGN)
-        nc.sync.dma_start(a_sb[:], a.rearrange("(p r) t -> p r t", r=PACK))
+        def sort_columns(dst, src, w, r_lo, r_hi):
+            nc.gpsimd.tensor_copy(
+                dst.rearrange("p (r b w) -> p r b w", r=PACK, w=w)[:, r_lo:r_hi],
+                src.rearrange("p (b r w) -> p r b w", r=PACK, w=w)[:, r_lo:r_hi],
+            )
 
-        y_t = [keep.tile([P, PACK, P], F32, name="y_t%d" % j, align_bytes=ALIGN) for j in range(E * BLOCKS)]
-        y_s = [keep.tile([P, T], F32, name="y_s%d" % r, align_bytes=ALIGN) for r in range(PACK)]
-        dh = [
-            keep.tile([P, 2 * T if r >= 2 else T], F32, name="dh%d" % r, tag="dh%d" % r, align_bytes=ALIGN)
-            for r in range(PACK)
-        ]
-        da = keep.tile([P, T, PACK], BF16, name="da", align_bytes=ALIGN)
+        def sort_words(e):
+            sort_columns(w2_w[e][:], w2_w_raw[e][:], RUN // 2, 0, PACK)
+
+        def sort_scales(e, r_lo, r_hi):
+            sort_columns(w2_s[e][:], w2_s_raw[:, e, :], RUN // 4, r_lo, r_hi)
+
+        y_raw = [tile([P, T], F32, "y_raw%d" % r) for r in range(PACK)]
+        y_s = [tile([P, T], F32, "y_s%d" % r) for r in range(PACK)]
+        dh = [tile([P, 2 * T if r >= 2 else T], F32, "dh%d" % r) for r in range(PACK)]
+        da = tile([P, T, PACK], BF16, "da")
 
         def da_plane(r, lo, hi):
             return da[:, lo:hi, r]
 
-        def sum_bank(b):
-            if b == HELD_BLOCK:
-                return psum.tile([P, H], F32, name="held", tag="spare")
-            return psum.tile([P, H], F32, name="acc", tag="acc", bufs=SUM_BANKS)
+        def sum_bank():
+            return psum.tile([P, HALF], F32, name="acc", tag="acc", bufs=SUM_BANKS)
 
-        def product(j):
-            e, b = divmod(j, BLOCKS)
-            acc = sum_bank(b)
+        def product(r, e):
+            acc = sum_bank()
             nc.tensor.matmul_mx(
                 out=acc[:],
-                lhsT=words_of(j * P, (j + 1) * P).bitcast(E5M2),
-                lhsT_scale=g_s[e][:, b * P : (b + 1) * P],
-                rhs=w2_w[e][:].bitcast(E2M1),
-                rhs_scale=w2_s[:, e, :].bitcast(U8),
+                lhsT=w2_w[e][:, r * P // 2 : (r + 1) * P // 2].bitcast(U8).bitcast(E2M1),
+                lhsT_scale=w2_s[e][:, r * P // 4 : (r + 1) * P // 4].bitcast(U8),
+                rhs=g_w[e][:].bitcast(E5M2),
+                rhs_scale=g_s[e][:],
                 start=True,
                 stop=True,
             )
             return acc
 
-        def weigh(j, acc, r_lo, r_hi):
-            nc.scalar.activation(
-                y_t[j][:, r_lo:r_hi, :],
-                acc[:].rearrange("p (m r) -> p r m", r=PACK)[:, r_lo:r_hi, :],
-                COPY,
-                scale=gate2[:, j : j + 1],
-            )
-
-        def turn(r, e, b_lo, b_hi):
-            if (r, e, b_lo) == (0, 0, 0) and b_hi == 1:
-                bank = psum.tile([P, C], F32, name="bank", tag="spare")
-            else:
-                bank = psum.tile([P, C], F32, name="bank", tag="bank", bufs=TURN_BANKS)
-            for b in range(b_lo, b_hi):
-                nc.tensor.transpose(bank[:, b * P : (b + 1) * P], y_t[BLOCKS * e + b][:, r, :], ident[:])
-            nc.scalar.copy(y_s[r][:, e * C + b_lo * P : e * C + b_hi * P], bank[:, b_lo * P : b_hi * P])
+        def weigh(acc, r, e, lo, hi):
+            cols = slice(e * C + lo, e * C + hi)
+            nc.scalar.activation(y_raw[r][:, cols], acc[:, lo:hi], COPY, scale=2.0)
+            nc.gpsimd.tensor_tensor(y_s[r][:, cols], y_raw[r][:, cols], gates[e][:, lo:hi], MULT)
 
         def scatter(r, lo, hi):
             nc.vector.tensor_copy(dh[r][:].indirect(slot_offsets(lo, hi)), y_s[r][:, lo:hi])
 
-        accs = [product(0)]
-        g_s.append(keep.tile([P, C], U8, name="g_s1", tag="first_words", align_bytes=ALIGN))
+        sort_words(0)
+        sort_scales(0, 0, 2)
+        g_s.append(tile([P, C], U8, "g_s1", "w2_w_raw0"))
         gather_scales(1)
-        w1_raw = keep.tile([P, PACK, K], F32, name="w1_raw", tag="scales_then_w1", align_bytes=ALIGN)
-        nc.sync.dma_start(w1_raw[:], w1t.rearrange("(p r) k -> p r k", r=PACK))
-
-        for r in range(2):
-            weigh(0, accs[0], r, r + 1)
-            turn(r, 0, 0, 1)
-            scatter(r, 0, P)
-        for b_lo, b_hi in ((1, 2), (2, BLOCKS)):
-            for j in range(b_lo, b_hi):
-                accs.append(product(j))
-                weigh(j, accs[j], 0, 2)
+        accs = [product(r, 0) for r in range(2)]
+        for lo, hi in ((0, P), (P, C)):
             for r in range(2):
-                turn(r, 0, b_lo, b_hi)
-                scatter(r, b_lo * P, b_hi * P)
-        for j in range(BLOCKS):
-            weigh(j, accs[j], 2, PACK)
-        for j in range(BLOCKS, E * BLOCKS):
-            accs.append(product(j))
-            weigh(j, accs[j], 0, 2)
+                weigh(accs[r], r, 0, lo, hi)
+                scatter(r, lo, hi)
+        sort_words(1)
+        sort_scales(1, 0, PACK)
+        for r in range(2):
+            weigh(product(r, 1), r, 1, 0, C)
+            scatter(r, C, T)
+        sort_scales(0, 2, PACK)
+        for r in range(2, PACK):
+            for e in range(E):
+                weigh(product(r, e), r, e, 0, C)
 
-        relu_a = []
+        a_sb = tile([P, PACK, T], F32, "a_sb", "words_then_a")
+        w1_raw = tile([P, PACK, K], F32, "w1_raw", "scales_then_w1")
+        for dst, src in ((a_sb, a), (w1_raw, w1t)):
+            rows = src.rearrange("(b r c) n -> r b c n", r=PACK, c=RUN)
+            for r in range(PACK):
+                nc.sync.dma_start(dst[:, r, :], rows[r])
+
+        relu_a = [tile([P, T], F32, "ra%d" % r) for r in range(LAST)]
         for r in range(LAST):
-            relu_a.append(keep.tile([P, T], F32, name="ra%d" % r, tag="ra%d" % r, align_bytes=ALIGN))
-            nc.gpsimd.tensor_scalar(relu_a[r][:], a_sb[:, r, :], F32_MAX, 0.0, MIN, MAX)
-        relu_pool = keep.tile([P, POOL_HI - POOL_LO], F32, name="relu_pool", align_bytes=ALIGN)
-        nc.gpsimd.tensor_scalar(relu_pool[:], a_sb[:, LAST, POOL_LO:POOL_HI], F32_MAX, 0.0, MIN, MAX)
-        w1_bf = keep.tile([P, K, PACK], BF16, name="w1_bf", align_bytes=ALIGN)
-        nc.gpsimd.tensor_scalar(w1_bf[:], w1_raw[:].rearrange("p r k -> p k r"), 1.0, 0.0, MULT, ADD)
+            nc.scalar.activation(relu_a[r][:], a_sb[:, r, :], RELU)
+        relu_pool = tile([P, POOL_HI - POOL_LO], F32, "relu_pool")
+        nc.scalar.activation(relu_pool[:], a_sb[:, LAST, POOL_LO:POOL_HI], RELU)
+        w1_bf = tile([P, K, PACK], BF16, "w1_bf")
+        nc.scalar.copy(w1_bf[:], w1_raw[:].rearrange("p r k -> p k r"))
 
         def multiply(r):
             nc.gpsimd.tensor_tensor(da_plane(r, 0, T), dh[r][:, 0:T], relu_a[r][:], MULT)
 
-        for r in range(2):
-            turn(r, 1, 0, BLOCKS)
-            scatter(r, C, T)
-            multiply(r)
-        for j in range(BLOCKS, E * BLOCKS):
-            weigh(j, accs[j], 2, PACK)
-        for r in range(2, PACK):
-            for e in range(E):
-                turn(r, e, 0, BLOCKS)
-            scatter(r, 0, T)
-            if r < LAST:
-                multiply(r)
+        multiply(0)
+        multiply(1)
+        scatter(2, 0, T)
+        multiply(2)
+        scatter(LAST, 0, T)
 
-        a_turned = keep.tile([P, T], F32, name="a_turned", tag="ra%d" % (LAST - 1), align_bytes=ALIGN)
+        a_turned = tile([P, T], F32, "a_turned", "ra%d" % (LAST - 1))
         relu_last = {}
         for lo, hi in ((0, POOL_LO), (POOL_HI, T)):
-            there = psum.tile([P, HALF], F32, name="acc", tag="acc", bufs=SUM_BANKS)
-            back = psum.tile([P, C], F32, name="bank", tag="bank", bufs=TURN_BANKS)
+            there = psum.tile([P, HALF], F32, name="there", tag="there", bufs=RELU_BANKS)
+            back = psum.tile([P, HALF], F32, name="back", tag="back", bufs=RELU_BANKS)
             for t in range(lo, hi, P):
                 nc.tensor.transpose(there[:, t - lo : t - lo + P], a_sb[:, LAST, t : t + P], ident[:])
             nc.scalar.activation(a_turned[:, lo:hi], there[:, 0 : hi - lo], RELU)
@@ -211,11 +190,11 @@ def tile_moe_sub_relu2_kernel(
             first = max(f for f in relu_last if f <= lo)
             return relu_last[first][:, lo - first : hi - first]
 
-        da_w = keep.tile([P, T], U32, name="da_w", align_bytes=ALIGN)
-        da_s = keep.tile([P, T], U8, name="da_s", align_bytes=ALIGN)
+        da_w = tile([P, T], U32, "da_w")
+        da_s = tile([P, T], U8, "da_s")
 
         def last_plane_dense(lo, hi):
-            dense = keep.tile([P, hi - lo], BF16, name="dense%d" % lo, align_bytes=ALIGN)
+            dense = tile([P, hi - lo], BF16, "dense%d" % lo)
             nc.vector.tensor_tensor(dense[:], dh[LAST][:, lo:hi], relu_in_psum(lo, hi), MULT)
             return dense
 
@@ -232,19 +211,19 @@ def tile_moe_sub_relu2_kernel(
                 in_=da[:, lo:hi, :].rearrange("p t r -> p (t r)"),
             )
 
-        w1_w = keep.tile([P, K], U32, name="w1_w", tag="dh%d" % (LAST - 1), align_bytes=ALIGN)
-        w1_s = keep.tile([P, K], U8, name="w1_s", align_bytes=ALIGN)
+        w1_w = tile([P, K], U32, "w1_w", "dh%d" % (LAST - 1))
+        w1_s = tile([P, K], U8, "w1_s")
         nc.vector.quantize_mx(out=w1_w[:].bitcast(E4M3), scales=w1_s[:], in_=w1_bf[:].rearrange("p k r -> p (k r)"))
         nc.gpsimd.tensor_tensor(
             da_plane(LAST, POOL_LO, POOL_HI), dh[LAST][:, POOL_LO:POOL_HI], relu_pool[:], MULT
         )
-        place(last_plane_dense(0, 176), 0, 176, 0)
-        last_plane_direct(176, POOL_LO)
-        dense_late = last_plane_dense(512, 896)
-        place(dense_late, 512, 768, 512)
-        place(dense_late, 768, 896, 512)
+        place(last_plane_dense(0, FIRST_EDGE), 0, FIRST_EDGE, 0)
+        last_plane_direct(FIRST_EDGE, POOL_LO)
+        dense_late = last_plane_dense(HALF, SECOND_EDGE)
+        place(dense_late, HALF, PARTS[1][1], HALF)
+        place(dense_late, PARTS[1][1], SECOND_EDGE, HALF)
         quantize_tokens(*PARTS[0])
-        last_plane_direct(896, T)
+        last_plane_direct(SECOND_EDGE, T)
         quantize_tokens(*PARTS[1])
         quantize_tokens(*PARTS[2])
 
@@ -252,7 +231,7 @@ def tile_moe_sub_relu2_kernel(
             cols = slice(h * HALF, (h + 1) * HALF)
             for kt in range(K // P):
                 rows = slice(kt * P, (kt + 1) * P)
-                acc = sum_bank(h * (K // P) + kt)
+                acc = sum_bank()
                 nc.tensor.matmul_mx(
                     out=acc[:],
                     lhsT=w1_w[:, rows].bitcast(E4M3),
@@ -262,7 +241,7 @@ def tile_moe_sub_relu2_kernel(
                     start=True,
                     stop=True,
                 )
-                res = keep.tile([P, HALF], F32, name="res%d_%d" % (h, kt), align_bytes=ALIGN)
+                res = tile([P, HALF], F32, "res%d_%d" % (h, kt))
                 copy = nc.scalar.copy if kt == 0 else nc.vector.tensor_copy
                 for lo in (0, HALF // 2):
                     hi = lo + HALF // 2

@@ -27,9 +27,10 @@ QUADRANTS = 4
 RUN = 8
 HALF = 512
 PARTS = ((0, 512), (512, 768), (768, 1024))
-POOL_LO, POOL_HI = 256, 512
-FIRST_EDGE = 176
-SECOND_EDGE = 896
+POOL_LO, POOL_HI = 272, 512
+FIRST_EDGE = 184
+SECOND_EDGE = 944
+RELU_BLOCKS = ((0, 1, 4, 5), (1, 2, 6, 7))
 ALIGN = 256
 SUM_BANKS = 4
 RELU_BANKS = 2
@@ -66,9 +67,11 @@ def tile_moe_sub_relu2_kernel(
         w2_scale_rows = w2t_scales[:, 0].rearrange("e b i -> b e i").bitcast(I32)
         for q in range(QUADRANTS):
             nc.sync.dma_start(w2_s_raw[32 * q : 32 * q + 4, :, :], w2_scale_rows[4 * q : 4 * q + 4, :, :])
-        nc.sync.dma_start(gates[0][:], gate[:, 0:C])
+        for lo, hi in ((0, P), (P, C)):
+            nc.sync.dma_start(gates[0][:, lo:hi], gate[:, lo:hi])
         nc.sync.dma_start(w2_w_raw[1][:], w2t_words[1, 0].bitcast(I32))
-        nc.sync.dma_start(gates[1][:], gate[:, C:T])
+        for lo in (0, C // 2):
+            nc.sync.dma_start(gates[1][:, lo : lo + C // 2], gate[:, C + lo : C + lo + C // 2])
         make_identity(nc, ident[:])
 
         g_w = [tile([P, C], U32, "g_w%d" % e) for e in range(E)]
@@ -175,34 +178,32 @@ def tile_moe_sub_relu2_kernel(
         scatter(LAST, 0, T)
 
         a_turned = tile([P, T], F32, "a_turned", "ra%d" % (LAST - 1))
-        relu_last = {}
-        for lo, hi in ((0, POOL_LO), (POOL_HI, T)):
+        relu_banks = []
+        for n, blocks in enumerate(RELU_BLOCKS):
             there = psum.tile([P, HALF], F32, name="there", tag="there", bufs=RELU_BANKS)
             back = psum.tile([P, HALF], F32, name="back", tag="back", bufs=RELU_BANKS)
-            for t in range(lo, hi, P):
-                nc.tensor.transpose(there[:, t - lo : t - lo + P], a_sb[:, LAST, t : t + P], ident[:])
-            nc.scalar.activation(a_turned[:, lo:hi], there[:, 0 : hi - lo], RELU)
-            for t in range(lo, hi, P):
-                nc.tensor.transpose(back[:, t - lo : t - lo + P], a_turned[:, t : t + P], ident[:])
-            relu_last[lo] = back
+            turned = a_turned[:, n * HALF : (n + 1) * HALF]
+            for m, b in enumerate(blocks):
+                nc.tensor.transpose(there[:, m * P : (m + 1) * P], a_sb[:, LAST, b * P : (b + 1) * P], ident[:])
+            nc.scalar.activation(turned, there[:], RELU)
+            for m in range(len(blocks)):
+                nc.tensor.transpose(back[:, m * P : (m + 1) * P], turned[:, m * P : (m + 1) * P], ident[:])
+            relu_banks.append(back)
 
-        def relu_in_psum(lo, hi):
-            first = max(f for f in relu_last if f <= lo)
-            return relu_last[first][:, lo - first : hi - first]
+        def relu_in_psum(n, lo, hi):
+            at = RELU_BLOCKS[n].index(lo // P) * P + lo % P
+            return relu_banks[n][:, at : at + hi - lo]
 
         da_w = tile([P, T], U32, "da_w")
         da_s = tile([P, T], U8, "da_s")
 
-        def last_plane_dense(lo, hi):
+        def dense_then_placed(n, lo, hi):
             dense = tile([P, hi - lo], BF16, "dense%d" % lo)
-            nc.vector.tensor_tensor(dense[:], dh[LAST][:, lo:hi], relu_in_psum(lo, hi), MULT)
-            return dense
+            nc.vector.tensor_tensor(dense[:], dh[LAST][:, lo:hi], relu_in_psum(n, lo, hi), MULT)
+            nc.scalar.copy(da_plane(LAST, lo, hi), dense[:])
 
-        def place(dense, lo, hi, first):
-            nc.scalar.copy(da_plane(LAST, lo, hi), dense[:, lo - first : hi - first])
-
-        def last_plane_direct(lo, hi):
-            nc.vector.tensor_tensor(da_plane(LAST, lo, hi), dh[LAST][:, lo:hi], relu_in_psum(lo, hi), MULT)
+        def direct(n, lo, hi):
+            nc.vector.tensor_tensor(da_plane(LAST, lo, hi), dh[LAST][:, lo:hi], relu_in_psum(n, lo, hi), MULT)
 
         def quantize_tokens(lo, hi):
             nc.vector.quantize_mx(
@@ -211,19 +212,24 @@ def tile_moe_sub_relu2_kernel(
                 in_=da[:, lo:hi, :].rearrange("p t r -> p (t r)"),
             )
 
-        w1_w = tile([P, K], U32, "w1_w", "dh%d" % (LAST - 1))
-        w1_s = tile([P, K], U8, "w1_s")
-        nc.vector.quantize_mx(out=w1_w[:].bitcast(E4M3), scales=w1_s[:], in_=w1_bf[:].rearrange("p k r -> p (k r)"))
+        def quantize_w1(kt, tag):
+            words = tile([P, P], U32, "w1_w%d" % kt, tag)
+            scales = tile([P, P], U8, "w1_s%d" % kt)
+            rows = w1_bf[:, kt * P : (kt + 1) * P, :].rearrange("p k r -> p (k r)")
+            nc.vector.quantize_mx(out=words[:].bitcast(E4M3), scales=scales[:], in_=rows)
+            return words, scales
+
+        w1_q = [quantize_w1(0, "dh%d" % (LAST - 1))]
         nc.gpsimd.tensor_tensor(
             da_plane(LAST, POOL_LO, POOL_HI), dh[LAST][:, POOL_LO:POOL_HI], relu_pool[:], MULT
         )
-        place(last_plane_dense(0, FIRST_EDGE), 0, FIRST_EDGE, 0)
-        last_plane_direct(FIRST_EDGE, POOL_LO)
-        dense_late = last_plane_dense(HALF, SECOND_EDGE)
-        place(dense_late, HALF, PARTS[1][1], HALF)
-        place(dense_late, PARTS[1][1], SECOND_EDGE, HALF)
+        dense_then_placed(0, 0, FIRST_EDGE)
+        dense_then_placed(0, *PARTS[1])
+        direct(1, FIRST_EDGE, POOL_LO)
+        dense_then_placed(1, PARTS[2][0], SECOND_EDGE)
         quantize_tokens(*PARTS[0])
-        last_plane_direct(SECOND_EDGE, T)
+        w1_q.append(quantize_w1(1, "dense0"))
+        direct(1, SECOND_EDGE, T)
         quantize_tokens(*PARTS[1])
         quantize_tokens(*PARTS[2])
 
@@ -234,8 +240,8 @@ def tile_moe_sub_relu2_kernel(
                 acc = sum_bank()
                 nc.tensor.matmul_mx(
                     out=acc[:],
-                    lhsT=w1_w[:, rows].bitcast(E4M3),
-                    lhsT_scale=w1_s[:, rows],
+                    lhsT=w1_q[kt][0][:].bitcast(E4M3),
+                    lhsT_scale=w1_q[kt][1][:],
                     rhs=da_w[:, cols].bitcast(E5M2),
                     rhs_scale=da_s[:, cols],
                     start=True,

@@ -27,10 +27,10 @@ QUADRANTS = 4
 RUN = 8
 HALF = 512
 PARTS = ((0, 512), (512, 768), (768, 1024))
-POOL_LO, POOL_HI = 272, 512
-FIRST_EDGE = 184
-SECOND_EDGE = 944
-RELU_BLOCKS = ((0, 1, 4, 5), (1, 2, 6, 7))
+POOL_LO, POOL_HI = 256, 512
+FIRST_EDGE = 144
+SECOND_EDGE = 896
+RELU_BLOCKS = ((0, 1, 4, 5), (1, 6, 7))
 ALIGN = 256
 SUM_BANKS = 4
 RELU_BANKS = 2
@@ -182,10 +182,11 @@ def tile_moe_sub_relu2_kernel(
         for n, blocks in enumerate(RELU_BLOCKS):
             there = psum.tile([P, HALF], F32, name="there", tag="there", bufs=RELU_BANKS)
             back = psum.tile([P, HALF], F32, name="back", tag="back", bufs=RELU_BANKS)
-            turned = a_turned[:, n * HALF : (n + 1) * HALF]
+            width = len(blocks) * P
+            turned = a_turned[:, n * HALF : n * HALF + width]
             for m, b in enumerate(blocks):
                 nc.tensor.transpose(there[:, m * P : (m + 1) * P], a_sb[:, LAST, b * P : (b + 1) * P], ident[:])
-            nc.scalar.activation(turned, there[:], RELU)
+            nc.scalar.activation(turned, there[:, 0:width], RELU)
             for m in range(len(blocks)):
                 nc.tensor.transpose(back[:, m * P : (m + 1) * P], turned[:, m * P : (m + 1) * P], ident[:])
             relu_banks.append(back)

@@ -1,7 +1,6 @@
 from contextlib import ExitStack
 
 import concourse.mybir as mybir
-from concourse.masks import make_identity
 
 K, T, E, C, H, N = 256, 1024, 2, 512, 512, 512
 FLOPS = 2 * N * H * E * C + 2 * H * K * T
@@ -16,24 +15,22 @@ E4M3 = mybir.dt.float8_e4m3fn_x4
 E5M2 = mybir.dt.float8_e5m2_x4
 E2M1 = mybir.dt.float4_e2m1fn_x4
 MULT = mybir.AluOpType.mult
+MIN = mybir.AluOpType.min
+MAX = mybir.AluOpType.max
 COPY = mybir.ActivationFunctionType.Copy
-RELU = mybir.ActivationFunctionType.Relu
 
 P = 128
 PACK = 4
-LAST = PACK - 1
 PER_COLUMN = 16
 QUADRANTS = 4
 RUN = 8
-HALF = 512
-PARTS = ((0, 512), (512, 768), (768, 1024))
-POOL_LO, POOL_HI = 256, 512
-FIRST_EDGE = 144
-SECOND_EDGE = 896
-RELU_BLOCKS = ((0, 1, 4, 5), (1, 6, 7))
+FIRST = 256
+SHARE = 640
+PIECE = 384
+CHUNK = 256
+F32_MAX = 3.4028234663852886e38
 ALIGN = 256
-SUM_BANKS = 4
-RELU_BANKS = 2
+BANKS = 8
 
 
 def tile_moe_sub_relu2_kernel(
@@ -48,12 +45,11 @@ def tile_moe_sub_relu2_kernel(
             return keep.tile(shape, dtype, name=name, tag=tag or name, align_bytes=ALIGN)
 
         offsets = tile([P, T // PER_COLUMN], U16, "offsets")
-        dy_w = tile([P, T], I32, "dy_w", "words_then_a")
-        dy_s = tile([P, T // 4], I32, "dy_s", "scales_then_w1")
+        dy_w = tile([P, T], I32, "dy_w")
+        dy_s = tile([P, T // 4], I32, "dy_s")
         w2_w_raw = [tile([P, H // 2], I32, "w2_w_raw%d" % e) for e in range(E)]
         w2_s_raw = tile([P, E, H // 4], I32, "w2_s_raw")
         gates = [tile([P, C], F32, "gate%d" % e) for e in range(E)]
-        ident = tile([P, P], F32, "ident")
 
         nc.gpsimd.memset(w2_s_raw[:], 0)
 
@@ -67,12 +63,23 @@ def tile_moe_sub_relu2_kernel(
         w2_scale_rows = w2t_scales[:, 0].rearrange("e b i -> b e i").bitcast(I32)
         for q in range(QUADRANTS):
             nc.sync.dma_start(w2_s_raw[32 * q : 32 * q + 4, :, :], w2_scale_rows[4 * q : 4 * q + 4, :, :])
-        for lo, hi in ((0, P), (P, C)):
+        for lo, hi in ((0, FIRST), (FIRST, C)):
             nc.sync.dma_start(gates[0][:, lo:hi], gate[:, lo:hi])
         nc.sync.dma_start(w2_w_raw[1][:], w2t_words[1, 0].bitcast(I32))
-        for lo in (0, C // 2):
-            nc.sync.dma_start(gates[1][:, lo : lo + C // 2], gate[:, C + lo : C + lo + C // 2])
-        make_identity(nc, ident[:])
+        nc.sync.dma_start(gates[1][:], gate[:, C:T])
+
+        w1_raw = tile([P, PACK, K], F32, "w1_raw")
+        w1_rows = w1t.rearrange("(b r c) n -> r b c n", r=PACK, c=RUN)
+        for r in range(PACK):
+            nc.sync.dma_start(w1_raw[:, r, :], w1_rows[r])
+        a_rows = a.rearrange("(b r c) n -> r b c n", r=PACK, c=RUN)
+
+        def load_a(r, tag=None):
+            plane = tile([P, T], F32, "a%d" % r, tag)
+            nc.sync.dma_start(plane[:], a_rows[r])
+            return plane
+
+        a_sb = {r: load_a(r) for r in (0, 1)}
 
         g_w = [tile([P, C], U32, "g_w%d" % e) for e in range(E)]
         g_s = [tile([P, C], U8, "g_s0")]
@@ -87,38 +94,36 @@ def tile_moe_sub_relu2_kernel(
         for e in range(E):
             nc.vector.tensor_copy(g_w[e][:], dy_w[:].bitcast(U32).indirect(slot_offsets(e * C, (e + 1) * C)))
 
-        w2_w = [tile([P, H // 2], I32, "w2_w%d" % e) for e in range(E)]
-        w2_s = [tile([P, H // 4], I32, "w2_s%d" % e) for e in range(E)]
+        w2_w, w2_s = {}, {}
 
-        def sort_columns(dst, src, w, r_lo, r_hi):
-            nc.gpsimd.tensor_copy(
-                dst.rearrange("p (r b w) -> p r b w", r=PACK, w=w)[:, r_lo:r_hi],
-                src.rearrange("p (b r w) -> p r b w", r=PACK, w=w)[:, r_lo:r_hi],
-            )
+        def sort_columns(name, src, w, planes):
+            dst = tile([P, len(planes), P // RUN, w], I32, name)
+            src = src.rearrange("p (b r w) -> p r b w", r=PACK, w=w)
+            nc.gpsimd.tensor_copy(dst[:], src[:, planes[0] : planes[-1] + 1])
+            return [dst[:, n].rearrange("p b w -> p (b w)").bitcast(U8) for n in range(len(planes))]
 
-        def sort_words(e):
-            sort_columns(w2_w[e][:], w2_w_raw[e][:], RUN // 2, 0, PACK)
+        def sort_w2(e, planes):
+            words = sort_columns("w2_w%d_%d" % (e, planes[0]), w2_w_raw[e][:], RUN // 2, planes)
+            scales = sort_columns("w2_s%d_%d" % (e, planes[0]), w2_s_raw[:, e, :], RUN // 4, planes)
+            for n, r in enumerate(planes):
+                w2_w[e, r], w2_s[e, r] = words[n], scales[n]
 
-        def sort_scales(e, r_lo, r_hi):
-            sort_columns(w2_s[e][:], w2_s_raw[:, e, :], RUN // 4, r_lo, r_hi)
+        y_s = [tile([P, SHARE if r == 0 else T], F32, "y_s%d" % r) for r in range(PACK)]
+        y_rest = tile([P, T - SHARE], F32, "y_rest")
+        dh = {0: tile([P, T], F32, "dh0")}
 
-        y_raw = [tile([P, T], F32, "y_raw%d" % r) for r in range(PACK)]
-        y_s = [tile([P, T], F32, "y_s%d" % r) for r in range(PACK)]
-        dh = [tile([P, 2 * T if r >= 2 else T], F32, "dh%d" % r) for r in range(PACK)]
-        da = tile([P, T, PACK], BF16, "da")
+        def sums(r, lo, hi):
+            return y_rest[:, lo - SHARE : hi - SHARE] if r == 0 and lo >= SHARE else y_s[r][:, lo:hi]
 
-        def da_plane(r, lo, hi):
-            return da[:, lo:hi, r]
-
-        def sum_bank():
-            return psum.tile([P, HALF], F32, name="acc", tag="acc", bufs=SUM_BANKS)
+        def bank(width):
+            return psum.tile([P, width], F32, name="acc", tag="acc", bufs=BANKS)
 
         def product(r, e):
-            acc = sum_bank()
+            acc = bank(C)
             nc.tensor.matmul_mx(
                 out=acc[:],
-                lhsT=w2_w[e][:, r * P // 2 : (r + 1) * P // 2].bitcast(U8).bitcast(E2M1),
-                lhsT_scale=w2_s[e][:, r * P // 4 : (r + 1) * P // 4].bitcast(U8),
+                lhsT=w2_w[e, r].bitcast(E2M1),
+                lhsT_scale=w2_s[e, r],
                 rhs=g_w[e][:].bitcast(E5M2),
                 rhs_scale=g_s[e][:],
                 start=True,
@@ -127,130 +132,103 @@ def tile_moe_sub_relu2_kernel(
             return acc
 
         def weigh(acc, r, e, lo, hi):
-            cols = slice(e * C + lo, e * C + hi)
-            nc.scalar.activation(y_raw[r][:, cols], acc[:, lo:hi], COPY, scale=2.0)
-            nc.gpsimd.tensor_tensor(y_s[r][:, cols], y_raw[r][:, cols], gates[e][:, lo:hi], MULT)
+            dst = sums(r, e * C + lo, e * C + hi)
+            nc.vector.scalar_tensor_tensor(dst, acc[:, lo:hi], 2.0, gates[e][:, lo:hi], MULT, MULT)
 
-        def scatter(r, lo, hi):
-            nc.vector.tensor_copy(dh[r][:].indirect(slot_offsets(lo, hi)), y_s[r][:, lo:hi])
+        def scatter_on_scalar(r, lo, hi):
+            nc.scalar.activation(dh[r][:].indirect(slot_offsets(lo, hi)), sums(r, lo, hi), COPY)
 
-        sort_words(0)
-        sort_scales(0, 0, 2)
-        g_s.append(tile([P, C], U8, "g_s1", "w2_w_raw0"))
+        def scatter_on_vector(r, lo, hi):
+            nc.vector.tensor_copy(dh[r][:].indirect(slot_offsets(lo, hi)), sums(r, lo, hi))
+
+        sort_w2(0, [0])
+        sort_w2(0, [1, 2, 3])
+        first = {r: product(r, 0) for r in range(PACK)}
+        weigh(first[0], 0, 0, 0, FIRST)
+        weigh(first[1], 1, 0, 0, C)
+        weigh(first[0], 0, 0, FIRST, C)
+        weigh(first[2], 2, 0, 0, C)
+        g_s.append(tile([P, C], U8, "g_s1", "g_s0"))
         gather_scales(1)
-        accs = [product(r, 0) for r in range(2)]
-        for lo, hi in ((0, P), (P, C)):
-            for r in range(2):
-                weigh(accs[r], r, 0, lo, hi)
-                scatter(r, lo, hi)
-        sort_words(1)
-        sort_scales(1, 0, PACK)
-        for r in range(2):
-            weigh(product(r, 1), r, 1, 0, C)
-            scatter(r, C, T)
-        sort_scales(0, 2, PACK)
-        for r in range(2, PACK):
-            for e in range(E):
-                weigh(product(r, e), r, e, 0, C)
+        sort_w2(1, [0, 1, 2, 3])
+        second = {r: product(r, 1) for r in (0, 1, 3, 2)}
+        weigh(second[0], 0, 1, 0, SHARE - C)
+        weigh(second[1], 1, 1, 0, C)
+        weigh(second[0], 0, 1, SHARE - C, C)
+        weigh(first[3], 3, 0, 0, C)
+        weigh(second[3], 3, 1, 0, C)
+        weigh(second[2], 2, 1, 0, C)
 
-        a_sb = tile([P, PACK, T], F32, "a_sb", "words_then_a")
-        w1_raw = tile([P, PACK, K], F32, "w1_raw", "scales_then_w1")
-        for dst, src in ((a_sb, a), (w1_raw, w1t)):
-            rows = src.rearrange("(b r c) n -> r b c n", r=PACK, c=RUN)
-            for r in range(PACK):
-                nc.sync.dma_start(dst[:, r, :], rows[r])
+        dh[1] = tile([P, T], F32, "dh1")
+        scatter_on_scalar(0, 0, FIRST)
+        scatter_on_scalar(1, 0, PIECE)
+        scatter_on_scalar(0, FIRST, SHARE)
+        scatter_on_scalar(1, PIECE, 2 * PIECE)
+        dh[3] = tile([P, T], F32, "dh3", "y_s0")
+        scatter_on_scalar(3, 0, T - 2 * PIECE)
+        scatter_on_scalar(1, 2 * PIECE, T)
+        scatter_on_scalar(3, T - 2 * PIECE, T - PIECE)
+        scatter_on_scalar(3, T - PIECE, T)
+        scatter_on_vector(0, SHARE, T)
+        dh[2] = tile([P, 2 * T], F32, "dh2", "y_rest")
+        scatter_on_vector(2, 0, T)
 
-        relu_a = [tile([P, T], F32, "ra%d" % r) for r in range(LAST)]
-        for r in range(LAST):
-            nc.scalar.activation(relu_a[r][:], a_sb[:, r, :], RELU)
-        relu_pool = tile([P, POOL_HI - POOL_LO], F32, "relu_pool")
-        nc.scalar.activation(relu_pool[:], a_sb[:, LAST, POOL_LO:POOL_HI], RELU)
         w1_bf = tile([P, K, PACK], BF16, "w1_bf")
-        nc.scalar.copy(w1_bf[:], w1_raw[:].rearrange("p r k -> p k r"))
+        nc.gpsimd.tensor_copy(w1_bf[:], w1_raw[:].rearrange("p r k -> p k r"))
+        chunks = [slice(lo, lo + CHUNK) for lo in range(0, T, CHUNK)]
+        pairs = [tile([P, 2, CHUNK, 2], BF16, "pairs%d" % n) for n in range(len(chunks))]
+        for r in range(2):
+            relu_a = tile([P, T], F32, "relu_a")
+            nc.gpsimd.tensor_scalar(relu_a[:], a_sb[r][:], F32_MAX, 0.0, MIN, MAX)
+            for n, cols in enumerate(chunks):
+                nc.gpsimd.tensor_tensor(pairs[n][:, 0, :, r], dh[r][:, cols], relu_a[:, cols], MULT)
+        a_sb[2] = load_a(2, "dy_w")
+        a_sb[3] = load_a(3, "a1")
 
-        def multiply(r):
-            nc.gpsimd.tensor_tensor(da_plane(r, 0, T), dh[r][:, 0:T], relu_a[r][:], MULT)
+        w1_w = tile([P, K], U32, "w1_w", "y_s2")
+        w1_s = tile([P, K], U8, "w1_s")
+        nc.vector.quantize_mx(
+            out=w1_w[:].bitcast(E4M3), scales=w1_s[:], in_=w1_bf[:].rearrange("p k r -> p (k r)")
+        )
 
-        multiply(0)
-        multiply(1)
-        scatter(2, 0, T)
-        multiply(2)
-        scatter(LAST, 0, T)
-
-        a_turned = tile([P, T], F32, "a_turned", "ra%d" % (LAST - 1))
-        relu_banks = []
-        for n, blocks in enumerate(RELU_BLOCKS):
-            there = psum.tile([P, HALF], F32, name="there", tag="there", bufs=RELU_BANKS)
-            back = psum.tile([P, HALF], F32, name="back", tag="back", bufs=RELU_BANKS)
-            width = len(blocks) * P
-            turned = a_turned[:, n * HALF : n * HALF + width]
-            for m, b in enumerate(blocks):
-                nc.tensor.transpose(there[:, m * P : (m + 1) * P], a_sb[:, LAST, b * P : (b + 1) * P], ident[:])
-            nc.scalar.activation(turned, there[:, 0:width], RELU)
-            for m in range(len(blocks)):
-                nc.tensor.transpose(back[:, m * P : (m + 1) * P], turned[:, m * P : (m + 1) * P], ident[:])
-            relu_banks.append(back)
-
-        def relu_in_psum(n, lo, hi):
-            at = RELU_BLOCKS[n].index(lo // P) * P + lo % P
-            return relu_banks[n][:, at : at + hi - lo]
-
-        da_w = tile([P, T], U32, "da_w")
-        da_s = tile([P, T], U8, "da_s")
-
-        def dense_then_placed(n, lo, hi):
-            dense = tile([P, hi - lo], BF16, "dense%d" % lo)
-            nc.vector.tensor_tensor(dense[:], dh[LAST][:, lo:hi], relu_in_psum(n, lo, hi), MULT)
-            nc.scalar.copy(da_plane(LAST, lo, hi), dense[:])
-
-        def direct(n, lo, hi):
-            nc.vector.tensor_tensor(da_plane(LAST, lo, hi), dh[LAST][:, lo:hi], relu_in_psum(n, lo, hi), MULT)
-
-        def quantize_tokens(lo, hi):
-            nc.vector.quantize_mx(
-                out=da_w[:, lo:hi].bitcast(E5M2),
-                scales=da_s[:, lo:hi],
-                in_=da[:, lo:hi, :].rearrange("p t r -> p (t r)"),
+        def multiply(r, n):
+            cols = chunks[n]
+            nc.vector.scalar_tensor_tensor(
+                pairs[n][:, 1, :, r - 2], a_sb[r][:, cols], 0.0, dh[r][:, cols], MAX, MULT
             )
 
-        def quantize_w1(kt, tag):
-            words = tile([P, P], U32, "w1_w%d" % kt, tag)
-            scales = tile([P, P], U8, "w1_s%d" % kt)
-            rows = w1_bf[:, kt * P : (kt + 1) * P, :].rearrange("p k r -> p (k r)")
-            nc.vector.quantize_mx(out=words[:].bitcast(E4M3), scales=scales[:], in_=rows)
-            return words, scales
+        def weave(n):
+            da = tile([P, CHUNK, PACK], BF16, "da%d" % n)
+            words = pairs[n][:].rearrange("p u t v -> p u (t v)").bitcast(F32)
+            copy = nc.vector.tensor_copy if n == 0 else nc.scalar.copy
+            copy(da[:].bitcast(F32), words.rearrange("p u t -> p t u"))
+            return da
 
-        w1_q = [quantize_w1(0, "dh%d" % (LAST - 1))]
-        nc.gpsimd.tensor_tensor(
-            da_plane(LAST, POOL_LO, POOL_HI), dh[LAST][:, POOL_LO:POOL_HI], relu_pool[:], MULT
-        )
-        dense_then_placed(0, 0, FIRST_EDGE)
-        dense_then_placed(0, *PARTS[1])
-        direct(1, FIRST_EDGE, POOL_LO)
-        dense_then_placed(1, PARTS[2][0], SECOND_EDGE)
-        quantize_tokens(*PARTS[0])
-        w1_q.append(quantize_w1(1, "dense0"))
-        direct(1, SECOND_EDGE, T)
-        quantize_tokens(*PARTS[1])
-        quantize_tokens(*PARTS[2])
-
-        for h in range(T // HALF):
-            cols = slice(h * HALF, (h + 1) * HALF)
+        def finish(n, da):
+            da_w = tile([P, CHUNK], U32, "da_w%d" % n)
+            da_s = tile([P, CHUNK], U8, "da_s%d" % n)
+            nc.vector.quantize_mx(
+                out=da_w[:].bitcast(E5M2), scales=da_s[:], in_=da[:].rearrange("p t r -> p (t r)")
+            )
             for kt in range(K // P):
                 rows = slice(kt * P, (kt + 1) * P)
-                acc = sum_bank()
+                acc = bank(CHUNK)
                 nc.tensor.matmul_mx(
                     out=acc[:],
-                    lhsT=w1_q[kt][0][:].bitcast(E4M3),
-                    lhsT_scale=w1_q[kt][1][:],
-                    rhs=da_w[:, cols].bitcast(E5M2),
-                    rhs_scale=da_s[:, cols],
+                    lhsT=w1_w[:, rows].bitcast(E4M3),
+                    lhsT_scale=w1_s[:, rows],
+                    rhs=da_w[:].bitcast(E5M2),
+                    rhs_scale=da_s[:],
                     start=True,
                     stop=True,
                 )
-                res = tile([P, HALF], F32, "res%d_%d" % (h, kt))
+                res = tile([P, CHUNK], F32, "res%d_%d" % (n, kt))
                 copy = nc.scalar.copy if kt == 0 else nc.vector.tensor_copy
-                for lo in (0, HALF // 2):
-                    hi = lo + HALF // 2
-                    copy(res[:, lo:hi], acc[:, lo:hi])
-                    nc.sync.dma_start(out[rows, h * HALF + lo : h * HALF + hi], res[:, lo:hi])
+                copy(res[:], acc[:])
+                nc.sync.dma_start(out[rows, chunks[n]], res[:])
+
+        for n in range(len(chunks)):
+            multiply(2, n)
+        for n in range(len(chunks)):
+            multiply(3, n)
+            finish(n, weave(n))

@@ -102,11 +102,15 @@ def tile_moe_sub_relu2_kernel(
             nc.gpsimd.tensor_copy(dst[:], src[:, planes[0] : planes[-1] + 1])
             return [dst[:, n].rearrange("p b w -> p (b w)").bitcast(U8) for n in range(len(planes))]
 
-        def sort_w2(e, planes):
+        def sort_words(e, planes):
             words = sort_columns("w2_w%d_%d" % (e, planes[0]), w2_w_raw[e][:], RUN // 2, planes)
+            for n, r in enumerate(planes):
+                w2_w[e, r] = words[n]
+
+        def sort_scales(e, planes):
             scales = sort_columns("w2_s%d_%d" % (e, planes[0]), w2_s_raw[:, e, :], RUN // 4, planes)
             for n, r in enumerate(planes):
-                w2_w[e, r], w2_s[e, r] = words[n], scales[n]
+                w2_s[e, r] = scales[n]
 
         y_s = [tile([P, SHARE if r == 0 else T], F32, "y_s%d" % r) for r in range(PACK)]
         y_rest = tile([P, T - SHARE], F32, "y_rest")
@@ -141,34 +145,37 @@ def tile_moe_sub_relu2_kernel(
         def scatter_on_vector(r, lo, hi):
             nc.vector.tensor_copy(dh[r][:].indirect(slot_offsets(lo, hi)), sums(r, lo, hi))
 
-        sort_w2(0, [0])
-        sort_w2(0, [1, 2, 3])
+        sort_words(0, [0, 1])
+        sort_words(0, [2, 3])
+        sort_scales(0, [0])
+        sort_scales(0, [1, 2, 3])
         first = {r: product(r, 0) for r in range(PACK)}
         weigh(first[0], 0, 0, 0, FIRST)
         weigh(first[1], 1, 0, 0, C)
-        weigh(first[0], 0, 0, FIRST, C)
-        weigh(first[2], 2, 0, 0, C)
-        g_s.append(tile([P, C], U8, "g_s1", "g_s0"))
+        g_s.append(tile([P, C], U8, "g_s1", "w2_w0_2"))
         gather_scales(1)
-        sort_w2(1, [0, 1, 2, 3])
+        weigh(first[0], 0, 0, FIRST, C)
+        sort_words(1, [0, 1, 2, 3])
+        sort_scales(1, [0, 1, 2, 3])
         second = {r: product(r, 1) for r in (0, 1, 3, 2)}
         weigh(second[0], 0, 1, 0, SHARE - C)
         weigh(second[1], 1, 1, 0, C)
         weigh(second[0], 0, 1, SHARE - C, C)
-        weigh(first[3], 3, 0, 0, C)
         weigh(second[3], 3, 1, 0, C)
+        weigh(first[2], 2, 0, 0, C)
+        weigh(first[3], 3, 0, 0, C)
         weigh(second[2], 2, 1, 0, C)
 
         dh[1] = tile([P, T], F32, "dh1")
+        dh[3] = tile([P, T], F32, "dh3")
         scatter_on_scalar(0, 0, FIRST)
-        scatter_on_scalar(1, 0, PIECE)
+        scatter_on_scalar(1, 0, T - 2 * PIECE)
         scatter_on_scalar(0, FIRST, SHARE)
-        scatter_on_scalar(1, PIECE, 2 * PIECE)
-        dh[3] = tile([P, T], F32, "dh3", "y_s0")
-        scatter_on_scalar(3, 0, T - 2 * PIECE)
-        scatter_on_scalar(1, 2 * PIECE, T)
-        scatter_on_scalar(3, T - 2 * PIECE, T - PIECE)
-        scatter_on_scalar(3, T - PIECE, T)
+        scatter_on_scalar(1, T - 2 * PIECE, T - PIECE)
+        scatter_on_scalar(3, 2 * PIECE, T)
+        scatter_on_scalar(1, T - PIECE, T)
+        scatter_on_scalar(3, 0, PIECE)
+        scatter_on_scalar(3, PIECE, 2 * PIECE)
         scatter_on_vector(0, SHARE, T)
         dh[2] = tile([P, 2 * T], F32, "dh2", "y_rest")
         scatter_on_vector(2, 0, T)
@@ -200,7 +207,7 @@ def tile_moe_sub_relu2_kernel(
         def weave(n):
             da = tile([P, CHUNK, PACK], BF16, "da%d" % n)
             words = pairs[n][:].rearrange("p u t v -> p u (t v)").bitcast(F32)
-            copy = nc.vector.tensor_copy if n == 0 else nc.scalar.copy
+            copy = nc.vector.tensor_copy if n == len(chunks) - 1 else nc.scalar.copy
             copy(da[:].bitcast(F32), words.rearrange("p u t -> p t u"))
             return da
 
@@ -223,7 +230,7 @@ def tile_moe_sub_relu2_kernel(
                     stop=True,
                 )
                 res = tile([P, CHUNK], F32, "res%d_%d" % (n, kt))
-                copy = nc.scalar.copy if kt == 0 else nc.vector.tensor_copy
+                copy = nc.vector.tensor_copy if kt == 1 and n >= len(chunks) // 2 else nc.scalar.copy
                 copy(res[:], acc[:])
                 nc.sync.dma_start(out[rows, chunks[n]], res[:])
 

@@ -15,6 +15,7 @@ E4M3 = mybir.dt.float8_e4m3fn_x4
 E5M2 = mybir.dt.float8_e5m2_x4
 E2M1 = mybir.dt.float4_e2m1fn_x4
 MULT = mybir.AluOpType.mult
+ADD = mybir.AluOpType.add
 MIN = mybir.AluOpType.min
 MAX = mybir.AluOpType.max
 COPY = mybir.ActivationFunctionType.Copy
@@ -25,7 +26,7 @@ PER_COLUMN = 16
 QUADRANTS = 4
 RUN = 8
 FIRST = 256
-SHARE = 640
+SHARE = 416
 PIECE = 384
 CHUNK = 256
 F32_MAX = 3.4028234663852886e38
@@ -60,11 +61,11 @@ def tile_moe_sub_relu2_kernel(
             queue.dma_start(dy_s[32 * q : 32 * q + 32, :], dy_scale_rows[4 * q : 4 * q + 4, :].partition_broadcast(8))
         nc.sync.dma_start(dy_w[:], dy_words[0].rearrange("p t d -> p (t d)").bitcast(I32))
         nc.sync.dma_start(w2_w_raw[0][:], w2t_words[0, 0].bitcast(I32))
+        nc.sync.dma_start(gates[0][:, 0:FIRST], gate[:, 0:FIRST])
         w2_scale_rows = w2t_scales[:, 0].rearrange("e b i -> b e i").bitcast(I32)
         for q in range(QUADRANTS):
             nc.sync.dma_start(w2_s_raw[32 * q : 32 * q + 4, :, :], w2_scale_rows[4 * q : 4 * q + 4, :, :])
-        for lo, hi in ((0, FIRST), (FIRST, C)):
-            nc.sync.dma_start(gates[0][:, lo:hi], gate[:, lo:hi])
+        nc.sync.dma_start(gates[0][:, FIRST:C], gate[:, FIRST:C])
         nc.sync.dma_start(w2_w_raw[1][:], w2t_words[1, 0].bitcast(I32))
         nc.sync.dma_start(gates[1][:], gate[:, C:T])
 
@@ -81,7 +82,7 @@ def tile_moe_sub_relu2_kernel(
 
         a_sb = {r: load_a(r) for r in (0, 1)}
 
-        g_w = [tile([P, C], U32, "g_w%d" % e) for e in range(E)]
+        g_w = [tile([P, C], U32, "g_w0")]
         g_s = [tile([P, C], U8, "g_s0")]
 
         def slot_offsets(lo, hi):
@@ -90,98 +91,99 @@ def tile_moe_sub_relu2_kernel(
         def gather_scales(e):
             nc.vector.tensor_copy(g_s[e][:], dy_s[:].bitcast(U8).indirect(slot_offsets(e * C, (e + 1) * C)))
 
+        def gather_words(e, lo, hi):
+            window = dy_w[:].bitcast(U32).indirect(slot_offsets(e * C + lo, e * C + hi))
+            nc.vector.tensor_copy(g_w[e][:, lo:hi], window)
+
         gather_scales(0)
-        for e in range(E):
-            nc.vector.tensor_copy(g_w[e][:], dy_w[:].bitcast(U32).indirect(slot_offsets(e * C, (e + 1) * C)))
+        gather_words(0, 0, FIRST)
+        gather_words(0, FIRST, C)
 
         w2_w, w2_s = {}, {}
+        sorters = (nc.scalar.copy, nc.gpsimd.tensor_copy)
 
-        def sort_columns(name, src, w, planes):
-            dst = tile([P, len(planes), P // RUN, w], I32, name)
-            src = src.rearrange("p (b r w) -> p r b w", r=PACK, w=w)
-            nc.gpsimd.tensor_copy(dst[:], src[:, planes[0] : planes[-1] + 1])
+        def sort_columns(name, copy, src, w, planes):
+            dst = tile([P, len(planes), P // RUN, w], U32, name)
+            src = src.bitcast(U32).rearrange("p (b r w) -> p r b w", r=PACK, w=w)
+            copy(dst[:], src[:, planes[0] : planes[-1] + 1])
             return [dst[:, n].rearrange("p b w -> p (b w)").bitcast(U8) for n in range(len(planes))]
 
         def sort_words(e, planes):
-            words = sort_columns("w2_w%d_%d" % (e, planes[0]), w2_w_raw[e][:], RUN // 2, planes)
+            words = sort_columns("w2_w%d_%d" % (e, planes[0]), sorters[e], w2_w_raw[e][:], RUN // 2, planes)
             for n, r in enumerate(planes):
                 w2_w[e, r] = words[n]
 
         def sort_scales(e, planes):
-            scales = sort_columns("w2_s%d_%d" % (e, planes[0]), w2_s_raw[:, e, :], RUN // 4, planes)
+            scales = sort_columns("w2_s%d_%d" % (e, planes[0]), sorters[e], w2_s_raw[:, e, :], RUN // 4, planes)
             for n, r in enumerate(planes):
                 w2_s[e, r] = scales[n]
 
-        y_s = [tile([P, SHARE if r == 0 else T], F32, "y_s%d" % r) for r in range(PACK)]
-        y_rest = tile([P, T - SHARE], F32, "y_rest")
-        dh = {0: tile([P, T], F32, "dh0")}
-
-        def sums(r, lo, hi):
-            return y_rest[:, lo - SHARE : hi - SHARE] if r == 0 and lo >= SHARE else y_s[r][:, lo:hi]
+        y_s = [tile([P, T], F32, "y_s%d" % r) for r in range(PACK)]
+        dh = [tile([P, 2 * T if r == 2 else T], F32, "dh%d" % r) for r in range(PACK)]
 
         def bank(width):
             return psum.tile([P, width], F32, name="acc", tag="acc", bufs=BANKS)
 
-        def product(r, e):
-            acc = bank(C)
+        def product(r, e, lo, hi):
+            acc = bank(hi - lo)
             nc.tensor.matmul_mx(
                 out=acc[:],
                 lhsT=w2_w[e, r].bitcast(E2M1),
                 lhsT_scale=w2_s[e, r],
-                rhs=g_w[e][:].bitcast(E5M2),
-                rhs_scale=g_s[e][:],
+                rhs=g_w[e][:, lo:hi].bitcast(E5M2),
+                rhs_scale=g_s[e][:, lo:hi],
                 start=True,
                 stop=True,
             )
             return acc
 
         def weigh(acc, r, e, lo, hi):
-            dst = sums(r, e * C + lo, e * C + hi)
-            nc.vector.scalar_tensor_tensor(dst, acc[:, lo:hi], 2.0, gates[e][:, lo:hi], MULT, MULT)
+            dst = y_s[r][:, e * C + lo : e * C + hi]
+            nc.vector.scalar_tensor_tensor(dst, acc[:], 2.0, gates[e][:, lo:hi], MULT, MULT)
 
         def scatter_on_scalar(r, lo, hi):
-            nc.scalar.activation(dh[r][:].indirect(slot_offsets(lo, hi)), sums(r, lo, hi), COPY)
+            nc.scalar.activation(dh[r][:].indirect(slot_offsets(lo, hi)), y_s[r][:, lo:hi], COPY)
 
         def scatter_on_vector(r, lo, hi):
-            nc.vector.tensor_copy(dh[r][:].indirect(slot_offsets(lo, hi)), sums(r, lo, hi))
+            nc.vector.tensor_copy(dh[r][:].indirect(slot_offsets(lo, hi)), y_s[r][:, lo:hi])
 
-        sort_words(0, [0, 1])
+        sort_words(0, [0])
+        sort_words(0, [1])
         sort_words(0, [2, 3])
         sort_scales(0, [0])
         sort_scales(0, [1, 2, 3])
-        first = {r: product(r, 0) for r in range(PACK)}
-        weigh(first[0], 0, 0, 0, FIRST)
+        halves = [product(0, 0, lo, hi) for lo, hi in ((0, FIRST), (FIRST, C))]
+        first = {r: product(r, 0, 0, C) for r in range(1, PACK)}
+        weigh(halves[0], 0, 0, 0, FIRST)
+        g_w.append(tile([P, C], U32, "g_w1", "w2_w0_0"))
+        gather_words(1, 0, C)
         weigh(first[1], 1, 0, 0, C)
         g_s.append(tile([P, C], U8, "g_s1", "w2_w0_2"))
         gather_scales(1)
-        weigh(first[0], 0, 0, FIRST, C)
+        weigh(halves[1], 0, 0, FIRST, C)
+        weigh(first[2], 2, 0, 0, C)
         sort_words(1, [0, 1, 2, 3])
         sort_scales(1, [0, 1, 2, 3])
-        second = {r: product(r, 1) for r in (0, 1, 3, 2)}
-        weigh(second[0], 0, 1, 0, SHARE - C)
-        weigh(second[1], 1, 1, 0, C)
-        weigh(second[0], 0, 1, SHARE - C, C)
-        weigh(second[3], 3, 1, 0, C)
-        weigh(first[2], 2, 0, 0, C)
+        second = {r: product(r, 1, 0, C) for r in (1, 3, 0, 2)}
+        for r in (1, 3, 0):
+            weigh(second[r], r, 1, 0, C)
+
+        scatter_on_scalar(0, 0, FIRST)
+        scatter_on_scalar(1, 0, PIECE)
+        scatter_on_scalar(0, FIRST, SHARE)
+        scatter_on_scalar(2, 0, FIRST)
+        scatter_on_scalar(1, PIECE, 2 * PIECE)
+        scatter_on_scalar(3, 2 * PIECE, T)
+        scatter_on_scalar(1, 2 * PIECE, T)
+        scatter_on_vector(0, SHARE, T)
         weigh(first[3], 3, 0, 0, C)
         weigh(second[2], 2, 1, 0, C)
-
-        dh[1] = tile([P, T], F32, "dh1")
-        dh[3] = tile([P, T], F32, "dh3")
-        scatter_on_scalar(0, 0, FIRST)
-        scatter_on_scalar(1, 0, T - 2 * PIECE)
-        scatter_on_scalar(0, FIRST, SHARE)
-        scatter_on_scalar(1, T - 2 * PIECE, T - PIECE)
-        scatter_on_scalar(3, 2 * PIECE, T)
-        scatter_on_scalar(1, T - PIECE, T)
         scatter_on_scalar(3, 0, PIECE)
         scatter_on_scalar(3, PIECE, 2 * PIECE)
-        scatter_on_vector(0, SHARE, T)
-        dh[2] = tile([P, 2 * T], F32, "dh2", "y_rest")
-        scatter_on_vector(2, 0, T)
+        scatter_on_vector(2, FIRST, T)
 
         w1_bf = tile([P, K, PACK], BF16, "w1_bf")
-        nc.gpsimd.tensor_copy(w1_bf[:], w1_raw[:].rearrange("p r k -> p k r"))
+        nc.gpsimd.tensor_scalar(w1_bf[:], w1_raw[:].rearrange("p r k -> p k r"), 1.0, 0.0, MULT, ADD)
         chunks = [slice(lo, lo + CHUNK) for lo in range(0, T, CHUNK)]
         pairs = [tile([P, 2, CHUNK, 2], BF16, "pairs%d" % n) for n in range(len(chunks))]
         for r in range(2):
@@ -190,9 +192,9 @@ def tile_moe_sub_relu2_kernel(
             for n, cols in enumerate(chunks):
                 nc.gpsimd.tensor_tensor(pairs[n][:, 0, :, r], dh[r][:, cols], relu_a[:, cols], MULT)
         a_sb[2] = load_a(2, "dy_w")
-        a_sb[3] = load_a(3, "a1")
+        a_sb[3] = load_a(3, "a0")
 
-        w1_w = tile([P, K], U32, "w1_w", "y_s2")
+        w1_w = tile([P, K], U32, "w1_w")
         w1_s = tile([P, K], U8, "w1_s")
         nc.vector.quantize_mx(
             out=w1_w[:].bitcast(E4M3), scales=w1_s[:], in_=w1_bf[:].rearrange("p k r -> p (k r)")
@@ -207,21 +209,22 @@ def tile_moe_sub_relu2_kernel(
         def weave(n):
             da = tile([P, CHUNK, PACK], BF16, "da%d" % n)
             words = pairs[n][:].rearrange("p u t v -> p u (t v)").bitcast(F32)
-            copy = nc.vector.tensor_copy if n == len(chunks) - 1 else nc.scalar.copy
+            copy = nc.scalar.copy
             copy(da[:].bitcast(F32), words.rearrange("p u t -> p t u"))
             return da
 
-        def finish(n, da):
+        def quantize(n, da):
             da_w = tile([P, CHUNK], U32, "da_w%d" % n)
             da_s = tile([P, CHUNK], U8, "da_s%d" % n)
             nc.vector.quantize_mx(
                 out=da_w[:].bitcast(E5M2), scales=da_s[:], in_=da[:].rearrange("p t r -> p (t r)")
             )
+            accs = []
             for kt in range(K // P):
                 rows = slice(kt * P, (kt + 1) * P)
-                acc = bank(CHUNK)
+                accs.append(bank(CHUNK))
                 nc.tensor.matmul_mx(
-                    out=acc[:],
+                    out=accs[kt][:],
                     lhsT=w1_w[:, rows].bitcast(E4M3),
                     lhsT_scale=w1_s[:, rows],
                     rhs=da_w[:].bitcast(E5M2),
@@ -229,13 +232,20 @@ def tile_moe_sub_relu2_kernel(
                     start=True,
                     stop=True,
                 )
-                res = tile([P, CHUNK], F32, "res%d_%d" % (n, kt))
-                copy = nc.vector.tensor_copy if kt == 1 and n >= len(chunks) // 2 else nc.scalar.copy
-                copy(res[:], acc[:])
-                nc.sync.dma_start(out[rows, chunks[n]], res[:])
+            return accs
+
+        def store(n, kt, acc):
+            res = tile([P, CHUNK], F32, "res%d_%d" % (n, kt))
+            copy = nc.vector.tensor_copy if (n, kt) in ((2, 0), (2, 1), (3, 0)) else nc.scalar.copy
+            copy(res[:], acc[:])
+            nc.sync.dma_start(out[kt * P : (kt + 1) * P, chunks[n]], res[:])
 
         for n in range(len(chunks)):
             multiply(2, n)
+        results = []
         for n in range(len(chunks)):
             multiply(3, n)
-            finish(n, weave(n))
+            results.append(quantize(n, weave(n)))
+        for n, accs in enumerate(results):
+            for kt, acc in enumerate(accs):
+                store(n, kt, acc)

@@ -26,8 +26,9 @@ PER_COLUMN = 16
 QUADRANTS = 4
 RUN = 8
 FIRST = 256
-SHARE = 416
+SHARE = 608
 PIECE = 384
+THIRD = 352
 CHUNK = 256
 F32_MAX = 3.4028234663852886e38
 ALIGN = 256
@@ -69,10 +70,6 @@ def tile_moe_sub_relu2_kernel(
         nc.sync.dma_start(w2_w_raw[1][:], w2t_words[1, 0].bitcast(I32))
         nc.sync.dma_start(gates[1][:], gate[:, C:T])
 
-        w1_raw = tile([P, PACK, K], F32, "w1_raw")
-        w1_rows = w1t.rearrange("(b r c) n -> r b c n", r=PACK, c=RUN)
-        for r in range(PACK):
-            nc.sync.dma_start(w1_raw[:, r, :], w1_rows[r])
         a_rows = a.rearrange("(b r c) n -> r b c n", r=PACK, c=RUN)
 
         def load_a(r, tag=None):
@@ -81,6 +78,10 @@ def tile_moe_sub_relu2_kernel(
             return plane
 
         a_sb = {r: load_a(r) for r in (0, 1)}
+        w1_raw = tile([P, PACK, K], F32, "w1_raw")
+        w1_rows = w1t.rearrange("(b r c) n -> r b c n", r=PACK, c=RUN)
+        for r in range(PACK):
+            nc.sync.dma_start(w1_raw[:, r, :], w1_rows[r])
 
         g_w = [tile([P, C], U32, "g_w0")]
         g_s = [tile([P, C], U8, "g_s0")]
@@ -118,8 +119,13 @@ def tile_moe_sub_relu2_kernel(
             for n, r in enumerate(planes):
                 w2_s[e, r] = scales[n]
 
-        y_s = [tile([P, T], F32, "y_s%d" % r) for r in range(PACK)]
-        dh = [tile([P, 2 * T if r == 2 else T], F32, "dh%d" % r) for r in range(PACK)]
+        y_s = [tile([P, T], F32, "y_s%d" % r) for r in range(PACK - 1)]
+        dh = [tile([P, T], F32, "dh%d" % r) for r in range(PACK)]
+
+        y_rest = []
+
+        def sums(r, lo, hi):
+            return y_rest[0][:, lo - SHARE : hi - SHARE] if r == 1 and lo >= SHARE else y_s[r][:, lo:hi]
 
         def bank(width):
             return psum.tile([P, width], F32, name="acc", tag="acc", bufs=BANKS)
@@ -138,14 +144,14 @@ def tile_moe_sub_relu2_kernel(
             return acc
 
         def weigh(acc, r, e, lo, hi):
-            dst = y_s[r][:, e * C + lo : e * C + hi]
-            nc.vector.scalar_tensor_tensor(dst, acc[:], 2.0, gates[e][:, lo:hi], MULT, MULT)
+            dst = sums(r, e * C + lo, e * C + hi)
+            nc.vector.scalar_tensor_tensor(dst, acc, 2.0, gates[e][:, lo:hi], MULT, MULT)
 
         def scatter_on_scalar(r, lo, hi):
             nc.scalar.activation(dh[r][:].indirect(slot_offsets(lo, hi)), y_s[r][:, lo:hi], COPY)
 
         def scatter_on_vector(r, lo, hi):
-            nc.vector.tensor_copy(dh[r][:].indirect(slot_offsets(lo, hi)), y_s[r][:, lo:hi])
+            nc.vector.tensor_copy(dh[r][:].indirect(slot_offsets(lo, hi)), sums(r, lo, hi))
 
         sort_words(0, [0])
         sort_words(0, [1])
@@ -154,51 +160,57 @@ def tile_moe_sub_relu2_kernel(
         sort_scales(0, [1, 2, 3])
         halves = [product(0, 0, lo, hi) for lo, hi in ((0, FIRST), (FIRST, C))]
         first = {r: product(r, 0, 0, C) for r in range(1, PACK)}
-        weigh(halves[0], 0, 0, 0, FIRST)
+        weigh(halves[0][:], 0, 0, 0, FIRST)
         g_w.append(tile([P, C], U32, "g_w1", "w2_w0_0"))
         gather_words(1, 0, C)
-        weigh(first[1], 1, 0, 0, C)
+        weigh(first[1][:], 1, 0, 0, C)
         g_s.append(tile([P, C], U8, "g_s1", "w2_w0_2"))
         gather_scales(1)
-        weigh(halves[1], 0, 0, FIRST, C)
-        weigh(first[2], 2, 0, 0, C)
+        weigh(halves[1][:], 0, 0, FIRST, C)
         sort_words(1, [0, 1, 2, 3])
         sort_scales(1, [0, 1, 2, 3])
-        second = {r: product(r, 1, 0, C) for r in (1, 3, 0, 2)}
-        for r in (1, 3, 0):
-            weigh(second[r], r, 1, 0, C)
+        second = {r: product(r, 1, 0, C) for r in (0, 1, 3, 2)}
+        edge = FIRST + PIECE - C
+        weigh(second[0][:, 0:edge], 0, 1, 0, edge)
+        weigh(first[2][:], 2, 0, 0, C)
+        weigh(second[1][:, 0 : SHARE - C], 1, 1, 0, SHARE - C)
+        weigh(second[0][:, edge:C], 0, 1, edge, C)
+        y_s.append(tile([P, T], F32, "y_s3", "w2_w1_0"))
+        weigh(second[3][:], 3, 1, 0, C)
+        weigh(first[3][:], 3, 0, 0, C)
+        weigh(second[2][:], 2, 1, 0, C)
+        y_rest.append(tile([P, T - SHARE], F32, "y_rest", "w2_w0_0"))
+        weigh(second[1][:, SHARE - C : C], 1, 1, SHARE - C, C)
 
-        scatter_on_scalar(0, 0, FIRST)
-        scatter_on_scalar(1, 0, PIECE)
-        scatter_on_scalar(0, FIRST, SHARE)
-        scatter_on_scalar(2, 0, FIRST)
-        scatter_on_scalar(1, PIECE, 2 * PIECE)
-        scatter_on_scalar(3, 2 * PIECE, T)
-        scatter_on_scalar(1, 2 * PIECE, T)
-        scatter_on_vector(0, SHARE, T)
-        weigh(first[3], 3, 0, 0, C)
-        weigh(second[2], 2, 1, 0, C)
-        scatter_on_scalar(3, 0, PIECE)
-        scatter_on_scalar(3, PIECE, 2 * PIECE)
-        scatter_on_vector(2, FIRST, T)
-
+        relu_a = [tile([P, T], F32, "relu_a%d" % r) for r in range(2)]
+        for r in range(2):
+            nc.gpsimd.tensor_scalar(relu_a[r][:], a_sb[r][:], F32_MAX, 0.0, MIN, MAX)
         w1_bf = tile([P, K, PACK], BF16, "w1_bf")
         nc.gpsimd.tensor_scalar(w1_bf[:], w1_raw[:].rearrange("p r k -> p k r"), 1.0, 0.0, MULT, ADD)
-        chunks = [slice(lo, lo + CHUNK) for lo in range(0, T, CHUNK)]
-        pairs = [tile([P, 2, CHUNK, 2], BF16, "pairs%d" % n) for n in range(len(chunks))]
-        for r in range(2):
-            relu_a = tile([P, T], F32, "relu_a")
-            nc.gpsimd.tensor_scalar(relu_a[:], a_sb[r][:], F32_MAX, 0.0, MIN, MAX)
-            for n, cols in enumerate(chunks):
-                nc.gpsimd.tensor_tensor(pairs[n][:, 0, :, r], dh[r][:, cols], relu_a[:, cols], MULT)
-        a_sb[2] = load_a(2, "dy_w")
-        a_sb[3] = load_a(3, "a0")
-
         w1_w = tile([P, K], U32, "w1_w")
         w1_s = tile([P, K], U8, "w1_s")
         nc.vector.quantize_mx(
             out=w1_w[:].bitcast(E4M3), scales=w1_s[:], in_=w1_bf[:].rearrange("p k r -> p (k r)")
         )
+
+        scatter_on_scalar(0, 0, FIRST)
+        scatter_on_scalar(1, 0, PIECE)
+        scatter_on_scalar(0, FIRST, FIRST + PIECE)
+        scatter_on_scalar(1, PIECE, SHARE)
+        scatter_on_scalar(0, FIRST + PIECE, T)
+        for lo, hi in ((2 * THIRD, T), (0, THIRD), (THIRD, 2 * THIRD)):
+            scatter_on_scalar(3, lo, hi)
+        scatter_on_vector(2, C, T)
+        scatter_on_vector(1, SHARE, T)
+        scatter_on_vector(2, 0, C)
+
+        chunks = [slice(lo, lo + CHUNK) for lo in range(0, T, CHUNK)]
+        pairs = [tile([P, 2, CHUNK, 2], BF16, "pairs%d" % n) for n in range(len(chunks))]
+        for r in range(2):
+            for n, cols in enumerate(chunks):
+                nc.gpsimd.tensor_tensor(pairs[n][:, 0, :, r], dh[r][:, cols], relu_a[r][:, cols], MULT)
+        a_sb[2] = load_a(2, "dy_w")
+        a_sb[3] = load_a(3, "a0")
 
         def multiply(r, n):
             cols = chunks[n]

@@ -27,8 +27,8 @@ QUADRANTS = 4
 RUN = 8
 FIRST = 256
 SHARE = 608
+HALF_SHARE = 320
 PIECE = 384
-THIRD = 352
 CHUNK = 256
 F32_MAX = 3.4028234663852886e38
 ALIGN = 256
@@ -119,13 +119,8 @@ def tile_moe_sub_relu2_kernel(
             for n, r in enumerate(planes):
                 w2_s[e, r] = scales[n]
 
-        y_s = [tile([P, T], F32, "y_s%d" % r) for r in range(PACK - 1)]
-        dh = [tile([P, T], F32, "dh%d" % r) for r in range(PACK)]
-
-        y_rest = []
-
-        def sums(r, lo, hi):
-            return y_rest[0][:, lo - SHARE : hi - SHARE] if r == 1 and lo >= SHARE else y_s[r][:, lo:hi]
+        y_s = {r: tile([P, T], F32, "y_s%d" % r) for r in (0, 1, 3)}
+        dh = [tile([P, 2 * T if r == 2 else T], F32, "dh%d" % r) for r in range(PACK)]
 
         def bank(width):
             return psum.tile([P, width], F32, name="acc", tag="acc", bufs=BANKS)
@@ -144,14 +139,14 @@ def tile_moe_sub_relu2_kernel(
             return acc
 
         def weigh(acc, r, e, lo, hi):
-            dst = sums(r, e * C + lo, e * C + hi)
+            dst = y_s[r][:, e * C + lo : e * C + hi]
             nc.vector.scalar_tensor_tensor(dst, acc, 2.0, gates[e][:, lo:hi], MULT, MULT)
 
         def scatter_on_scalar(r, lo, hi):
             nc.scalar.activation(dh[r][:].indirect(slot_offsets(lo, hi)), y_s[r][:, lo:hi], COPY)
 
         def scatter_on_vector(r, lo, hi):
-            nc.vector.tensor_copy(dh[r][:].indirect(slot_offsets(lo, hi)), sums(r, lo, hi))
+            nc.vector.tensor_copy(dh[r][:].indirect(slot_offsets(lo, hi)), y_s[r][:, lo:hi])
 
         sort_words(0, [0])
         sort_words(0, [1])
@@ -169,18 +164,18 @@ def tile_moe_sub_relu2_kernel(
         weigh(halves[1][:], 0, 0, FIRST, C)
         sort_words(1, [0, 1, 2, 3])
         sort_scales(1, [0, 1, 2, 3])
-        second = {r: product(r, 1, 0, C) for r in (0, 1, 3, 2)}
-        edge = FIRST + PIECE - C
-        weigh(second[0][:, 0:edge], 0, 1, 0, edge)
-        weigh(first[2][:], 2, 0, 0, C)
-        weigh(second[1][:, 0 : SHARE - C], 1, 1, 0, SHARE - C)
-        weigh(second[0][:, edge:C], 0, 1, edge, C)
-        y_s.append(tile([P, T], F32, "y_s3", "w2_w1_0"))
-        weigh(second[3][:], 3, 1, 0, C)
+        second = {r: product(r, 1, 0, hi) for r, hi in ((0, FIRST), (1, C))}
+        rest = product(0, 1, FIRST, C)
+        for r in (3, 2):
+            second[r] = product(r, 1, 0, C)
+        weigh(second[0][:], 0, 1, 0, FIRST)
         weigh(first[3][:], 3, 0, 0, C)
+        weigh(second[1][:], 1, 1, 0, C)
+        weigh(rest[:], 0, 1, FIRST, C)
+        weigh(second[3][:], 3, 1, 0, C)
+        y_s[2] = tile([P, T], F32, "y_s2", "w2_w0_0")
+        weigh(first[2][:], 2, 0, 0, C)
         weigh(second[2][:], 2, 1, 0, C)
-        y_rest.append(tile([P, T - SHARE], F32, "y_rest", "w2_w0_0"))
-        weigh(second[1][:, SHARE - C : C], 1, 1, SHARE - C, C)
 
         relu_a = [tile([P, T], F32, "relu_a%d" % r) for r in range(2)]
         for r in range(2):
@@ -196,13 +191,13 @@ def tile_moe_sub_relu2_kernel(
         scatter_on_scalar(0, 0, FIRST)
         scatter_on_scalar(1, 0, PIECE)
         scatter_on_scalar(0, FIRST, FIRST + PIECE)
-        scatter_on_scalar(1, PIECE, SHARE)
-        scatter_on_scalar(0, FIRST + PIECE, T)
-        for lo, hi in ((2 * THIRD, T), (0, THIRD), (THIRD, 2 * THIRD)):
-            scatter_on_scalar(3, lo, hi)
-        scatter_on_vector(2, C, T)
-        scatter_on_vector(1, SHARE, T)
-        scatter_on_vector(2, 0, C)
+        scatter_on_scalar(1, PIECE, T - PIECE)
+        scatter_on_scalar(0, T - PIECE, T)
+        scatter_on_scalar(1, T - PIECE, T)
+        scatter_on_vector(3, SHARE, T)
+        scatter_on_vector(2, 0, T)
+        scatter_on_scalar(3, 0, SHARE - HALF_SHARE)
+        scatter_on_scalar(3, SHARE - HALF_SHARE, SHARE)
 
         chunks = [slice(lo, lo + CHUNK) for lo in range(0, T, CHUNK)]
         pairs = [tile([P, 2, CHUNK, 2], BF16, "pairs%d" % n) for n in range(len(chunks))]

@@ -119,7 +119,7 @@ def tile_moe_sub_relu2_kernel(
             for n, r in enumerate(planes):
                 w2_s[e, r] = scales[n]
 
-        y_s = {r: tile([P, T], F32, "y_s%d" % r) for r in (0, 1, 3)}
+        y_s = [tile([P, T], F32, "y_s%d" % r) for r in range(PACK)]
         dh = [tile([P, 2 * T if r == 2 else T], F32, "dh%d" % r) for r in range(PACK)]
 
         def bank(width):
@@ -170,11 +170,10 @@ def tile_moe_sub_relu2_kernel(
             second[r] = product(r, 1, 0, C)
         weigh(second[0][:], 0, 1, 0, FIRST)
         weigh(first[3][:], 3, 0, 0, C)
+        weigh(first[2][:], 2, 0, 0, C)
         weigh(second[1][:], 1, 1, 0, C)
         weigh(rest[:], 0, 1, FIRST, C)
         weigh(second[3][:], 3, 1, 0, C)
-        y_s[2] = tile([P, T], F32, "y_s2", "w2_w0_0")
-        weigh(first[2][:], 2, 0, 0, C)
         weigh(second[2][:], 2, 1, 0, C)
 
         relu_a = [tile([P, T], F32, "relu_a%d" % r) for r in range(2)]
@@ -200,23 +199,23 @@ def tile_moe_sub_relu2_kernel(
         scatter_on_scalar(3, SHARE - HALF_SHARE, SHARE)
 
         chunks = [slice(lo, lo + CHUNK) for lo in range(0, T, CHUNK)]
-        pairs = [tile([P, 2, CHUNK, 2], BF16, "pairs%d" % n) for n in range(len(chunks))]
+        pairs = tile([P, 2, T, 2], BF16, "pairs")
         for r in range(2):
-            for n, cols in enumerate(chunks):
-                nc.gpsimd.tensor_tensor(pairs[n][:, 0, :, r], dh[r][:, cols], relu_a[r][:, cols], MULT)
+            nc.gpsimd.tensor_tensor(pairs[:, 0, :, r], dh[r][:], relu_a[r][:], MULT)
         a_sb[2] = load_a(2, "dy_w")
-        a_sb[3] = load_a(3, "a0")
+        a_last = []
+        for r, (lo, hi) in enumerate(((0, T - CHUNK), (T - CHUNK, T))):
+            part = tile([P, hi - lo], F32, "a3_%d" % lo, "relu_a%d" % r)
+            nc.sync.dma_start(part[:], a_rows[3][:, :, lo:hi])
+            a_last.extend(part[:, at : at + CHUNK] for at in range(0, hi - lo, CHUNK))
 
-        def multiply(r, n):
-            cols = chunks[n]
-            nc.vector.scalar_tensor_tensor(
-                pairs[n][:, 1, :, r - 2], a_sb[r][:, cols], 0.0, dh[r][:, cols], MAX, MULT
-            )
+        def multiply(r, cols, a_cols):
+            nc.vector.scalar_tensor_tensor(pairs[:, 1, cols, r - 2], a_cols, 0.0, dh[r][:, cols], MAX, MULT)
 
         def weave(n):
             da = tile([P, CHUNK, PACK], BF16, "da%d" % n)
-            words = pairs[n][:].rearrange("p u t v -> p u (t v)").bitcast(F32)
-            copy = nc.scalar.copy
+            words = pairs[:].rearrange("p u t v -> p u (t v)").bitcast(F32)[:, :, chunks[n]]
+            copy = nc.vector.tensor_copy if n == len(chunks) - 1 else nc.scalar.copy
             copy(da[:].bitcast(F32), words.rearrange("p u t -> p t u"))
             return da
 
@@ -243,15 +242,14 @@ def tile_moe_sub_relu2_kernel(
 
         def store(n, kt, acc):
             res = tile([P, CHUNK], F32, "res%d_%d" % (n, kt))
-            copy = nc.vector.tensor_copy if (n, kt) in ((2, 0), (2, 1), (3, 0)) else nc.scalar.copy
+            copy = nc.vector.tensor_copy if (n, kt) in ((1, 0), (3, 0)) else nc.scalar.copy
             copy(res[:], acc[:])
             nc.sync.dma_start(out[kt * P : (kt + 1) * P, chunks[n]], res[:])
 
-        for n in range(len(chunks)):
-            multiply(2, n)
+        multiply(2, slice(0, T), a_sb[2][:])
         results = []
         for n in range(len(chunks)):
-            multiply(3, n)
+            multiply(3, chunks[n], a_last[n])
             results.append(quantize(n, weave(n)))
         for n, accs in enumerate(results):
             for kt, acc in enumerate(accs):

@@ -26,8 +26,8 @@ PER_COLUMN = 16
 QUADRANTS = 4
 RUN = 8
 FIRST = 256
-SHARE = 608
-HALF_SHARE = 320
+SHARE = 576
+HALF_SHARE = 288
 PIECE = 384
 CHUNK = 256
 F32_MAX = 3.4028234663852886e38
@@ -77,13 +77,14 @@ def tile_moe_sub_relu2_kernel(
             nc.sync.dma_start(plane[:], a_rows[r])
             return plane
 
-        a_sb = {r: load_a(r) for r in (0, 1)}
         w1_raw = tile([P, PACK, K], F32, "w1_raw")
         w1_rows = w1t.rearrange("(b r c) n -> r b c n", r=PACK, c=RUN)
         for r in range(PACK):
             nc.sync.dma_start(w1_raw[:, r, :], w1_rows[r])
+        a_sb = {r: load_a(r) for r in (0, 1)}
 
-        g_w = [tile([P, C], U32, "g_w0")]
+        ring = tile([P, C + FIRST], U32, "g_w")
+        g_w = [ring[:, FIRST : FIRST + C], ring[:, 0:C]]
         g_s = [tile([P, C], U8, "g_s0")]
 
         def slot_offsets(lo, hi):
@@ -99,6 +100,7 @@ def tile_moe_sub_relu2_kernel(
         gather_scales(0)
         gather_words(0, 0, FIRST)
         gather_words(0, FIRST, C)
+        gather_words(1, 0, FIRST)
 
         w2_w, w2_s = {}, {}
         sorters = (nc.scalar.copy, nc.gpsimd.tensor_copy)
@@ -119,8 +121,8 @@ def tile_moe_sub_relu2_kernel(
             for n, r in enumerate(planes):
                 w2_s[e, r] = scales[n]
 
-        y_s = [tile([P, T], F32, "y_s%d" % r) for r in range(PACK)]
-        dh = [tile([P, 2 * T if r == 2 else T], F32, "dh%d" % r) for r in range(PACK)]
+        y_s = {r: tile([P, T], F32, "y_s%d" % r) for r in (0, 1, 3)}
+        dh = {r: tile([P, 2 * T if r == 2 else T], F32, "dh%d" % r) for r in range(PACK - 1)}
 
         def bank(width):
             return psum.tile([P, width], F32, name="acc", tag="acc", bufs=BANKS)
@@ -149,18 +151,16 @@ def tile_moe_sub_relu2_kernel(
             nc.vector.tensor_copy(dh[r][:].indirect(slot_offsets(lo, hi)), y_s[r][:, lo:hi])
 
         sort_words(0, [0])
-        sort_words(0, [1])
-        sort_words(0, [2, 3])
+        sort_words(0, [1, 2, 3])
         sort_scales(0, [0])
         sort_scales(0, [1, 2, 3])
         halves = [product(0, 0, lo, hi) for lo, hi in ((0, FIRST), (FIRST, C))]
         first = {r: product(r, 0, 0, C) for r in range(1, PACK)}
         weigh(halves[0][:], 0, 0, 0, FIRST)
-        g_w.append(tile([P, C], U32, "g_w1", "w2_w0_0"))
-        gather_words(1, 0, C)
-        weigh(first[1][:], 1, 0, 0, C)
-        g_s.append(tile([P, C], U8, "g_s1", "w2_w0_2"))
+        g_s.append(tile([P, C], U8, "g_s1", "w2_w0_0"))
         gather_scales(1)
+        weigh(first[1][:], 1, 0, 0, C)
+        gather_words(1, FIRST, C)
         weigh(halves[1][:], 0, 0, FIRST, C)
         sort_words(1, [0, 1, 2, 3])
         sort_scales(1, [0, 1, 2, 3])
@@ -170,15 +170,10 @@ def tile_moe_sub_relu2_kernel(
             second[r] = product(r, 1, 0, C)
         weigh(second[0][:], 0, 1, 0, FIRST)
         weigh(first[3][:], 3, 0, 0, C)
-        weigh(first[2][:], 2, 0, 0, C)
         weigh(second[1][:], 1, 1, 0, C)
         weigh(rest[:], 0, 1, FIRST, C)
         weigh(second[3][:], 3, 1, 0, C)
-        weigh(second[2][:], 2, 1, 0, C)
 
-        relu_a = [tile([P, T], F32, "relu_a%d" % r) for r in range(2)]
-        for r in range(2):
-            nc.gpsimd.tensor_scalar(relu_a[r][:], a_sb[r][:], F32_MAX, 0.0, MIN, MAX)
         w1_bf = tile([P, K, PACK], BF16, "w1_bf")
         nc.gpsimd.tensor_scalar(w1_bf[:], w1_raw[:].rearrange("p r k -> p k r"), 1.0, 0.0, MULT, ADD)
         w1_w = tile([P, K], U32, "w1_w")
@@ -186,6 +181,16 @@ def tile_moe_sub_relu2_kernel(
         nc.vector.quantize_mx(
             out=w1_w[:].bitcast(E4M3), scales=w1_s[:], in_=w1_bf[:].rearrange("p k r -> p (k r)")
         )
+
+        y_s[2] = tile([P, T], F32, "y_s2", "w1_raw")
+        weigh(first[2][:], 2, 0, 0, C)
+        weigh(second[2][:], 2, 1, 0, C)
+        dh[3] = tile([P, T], F32, "dh3", "w1_bf")
+        relu_tags = ("gate1", "a0")
+        relu_a = []
+        for r in range(2):
+            relu_a.append(tile([P, T], F32, "relu_a%d" % r, relu_tags[r]))
+            nc.gpsimd.tensor_scalar(relu_a[r][:], a_sb[r][:], F32_MAX, 0.0, MIN, MAX)
 
         scatter_on_scalar(0, 0, FIRST)
         scatter_on_scalar(1, 0, PIECE)
@@ -205,7 +210,7 @@ def tile_moe_sub_relu2_kernel(
         a_sb[2] = load_a(2, "dy_w")
         a_last = []
         for r, (lo, hi) in enumerate(((0, T - CHUNK), (T - CHUNK, T))):
-            part = tile([P, hi - lo], F32, "a3_%d" % lo, "relu_a%d" % r)
+            part = tile([P, hi - lo], F32, "a3_%d" % lo, relu_tags[r])
             nc.sync.dma_start(part[:], a_rows[3][:, :, lo:hi])
             a_last.extend(part[:, at : at + CHUNK] for at in range(0, hi - lo, CHUNK))
 

@@ -27,7 +27,7 @@ QUADRANTS = 4
 RUN = 8
 FIRST = 256
 SHARE = 576
-HALF_SHARE = 288
+OVERLAP = 16
 PIECE = 384
 CHUNK = 256
 F32_MAX = 3.4028234663852886e38
@@ -121,23 +121,25 @@ def tile_moe_sub_relu2_kernel(
             for n, r in enumerate(planes):
                 w2_s[e, r] = scales[n]
 
-        y_s = {r: tile([P, T], F32, "y_s%d" % r) for r in (0, 1, 3)}
-        dh = {r: tile([P, 2 * T if r == 2 else T], F32, "dh%d" % r) for r in range(PACK - 1)}
+        y_s = [tile([P, T], F32, "y_s%d" % r) for r in range(PACK)]
+        dh = [tile([P, 2 * T if r == 2 else T], F32, "dh%d" % r) for r in range(PACK)]
+
 
         def bank(width):
             return psum.tile([P, width], F32, name="acc", tag="acc", bufs=BANKS)
 
-        def product(r, e, lo, hi):
-            acc = bank(hi - lo)
-            nc.tensor.matmul_mx(
-                out=acc[:],
-                lhsT=w2_w[e, r].bitcast(E2M1),
-                lhsT_scale=w2_s[e, r],
-                rhs=g_w[e][:, lo:hi].bitcast(E5M2),
-                rhs_scale=g_s[e][:, lo:hi],
-                start=True,
-                stop=True,
-            )
+        def product(r, e, *edges):
+            acc = bank(edges[-1] - edges[0])
+            for lo, hi in zip(edges, edges[1:]):
+                nc.tensor.matmul_mx(
+                    out=acc[:, lo - edges[0] : hi - edges[0]],
+                    lhsT=w2_w[e, r].bitcast(E2M1),
+                    lhsT_scale=w2_s[e, r],
+                    rhs=g_w[e][:, lo:hi].bitcast(E5M2),
+                    rhs_scale=g_s[e][:, lo:hi],
+                    start=True,
+                    stop=True,
+                )
             return acc
 
         def weigh(acc, r, e, lo, hi):
@@ -164,15 +166,35 @@ def tile_moe_sub_relu2_kernel(
         weigh(halves[1][:], 0, 0, FIRST, C)
         sort_words(1, [0, 1, 2, 3])
         sort_scales(1, [0, 1, 2, 3])
-        second = {r: product(r, 1, 0, hi) for r, hi in ((0, FIRST), (1, C))}
-        rest = product(0, 1, FIRST, C)
+        weigh(product(0, 1, 0, P)[:], 0, 1, 0, P)
+        second = {r: product(r, 1, 0, C) for r in (1, 3)}
+        rest = product(0, 1, P, FIRST, C)
+        second[2] = product(2, 1, 0, C)
         for r in (3, 2):
-            second[r] = product(r, 1, 0, C)
-        weigh(second[0][:], 0, 1, 0, FIRST)
-        weigh(first[3][:], 3, 0, 0, C)
-        weigh(second[1][:], 1, 1, 0, C)
-        weigh(rest[:], 0, 1, FIRST, C)
-        weigh(second[3][:], 3, 1, 0, C)
+            weigh(first[r][:], r, 0, 0, C)
+        for r in (1, 3):
+            weigh(second[r][:], r, 1, 0, C)
+        weigh(rest[:], 0, 1, P, C)
+        weigh(second[2][:], 2, 1, 0, C)
+        relus = tile([P, 2 * T - OVERLAP], F32, "relus")
+        relu_a = [relus[:, 0:T], relus[:, T - OVERLAP :]]
+
+        def relu(r, lo, hi):
+            nc.gpsimd.tensor_scalar(relu_a[r][:, lo:hi], a_sb[r][:, lo:hi], F32_MAX, 0.0, MIN, MAX)
+
+        relu(0, 0, T)
+        relu(1, OVERLAP, T)
+
+        scatter_on_scalar(0, 0, FIRST)
+        scatter_on_scalar(1, 0, T - 2 * PIECE)
+        scatter_on_scalar(0, FIRST, SHARE)
+        scatter_on_scalar(1, T - 2 * PIECE, T - PIECE)
+        scatter_on_scalar(3, 2 * PIECE, T)
+        scatter_on_scalar(1, T - PIECE, T)
+        scatter_on_scalar(3, 0, PIECE)
+        scatter_on_scalar(3, PIECE, 2 * PIECE)
+        scatter_on_vector(0, SHARE, T)
+        scatter_on_vector(2, 0, T)
 
         w1_bf = tile([P, K, PACK], BF16, "w1_bf")
         nc.gpsimd.tensor_scalar(w1_bf[:], w1_raw[:].rearrange("p r k -> p k r"), 1.0, 0.0, MULT, ADD)
@@ -182,35 +204,15 @@ def tile_moe_sub_relu2_kernel(
             out=w1_w[:].bitcast(E4M3), scales=w1_s[:], in_=w1_bf[:].rearrange("p k r -> p (k r)")
         )
 
-        y_s[2] = tile([P, T], F32, "y_s2", "w1_raw")
-        weigh(first[2][:], 2, 0, 0, C)
-        weigh(second[2][:], 2, 1, 0, C)
-        dh[3] = tile([P, T], F32, "dh3", "w1_bf")
-        relu_tags = ("gate1", "a0")
-        relu_a = []
-        for r in range(2):
-            relu_a.append(tile([P, T], F32, "relu_a%d" % r, relu_tags[r]))
-            nc.gpsimd.tensor_scalar(relu_a[r][:], a_sb[r][:], F32_MAX, 0.0, MIN, MAX)
-
-        scatter_on_scalar(0, 0, FIRST)
-        scatter_on_scalar(1, 0, PIECE)
-        scatter_on_scalar(0, FIRST, FIRST + PIECE)
-        scatter_on_scalar(1, PIECE, T - PIECE)
-        scatter_on_scalar(0, T - PIECE, T)
-        scatter_on_scalar(1, T - PIECE, T)
-        scatter_on_vector(3, SHARE, T)
-        scatter_on_vector(2, 0, T)
-        scatter_on_scalar(3, 0, SHARE - HALF_SHARE)
-        scatter_on_scalar(3, SHARE - HALF_SHARE, SHARE)
-
         chunks = [slice(lo, lo + CHUNK) for lo in range(0, T, CHUNK)]
         pairs = tile([P, 2, T, 2], BF16, "pairs")
-        for r in range(2):
-            nc.gpsimd.tensor_tensor(pairs[:, 0, :, r], dh[r][:], relu_a[r][:], MULT)
+        nc.gpsimd.tensor_tensor(pairs[:, 0, :, 0], dh[0][:], relu_a[0], MULT)
+        relu(1, 0, OVERLAP)
+        nc.gpsimd.tensor_tensor(pairs[:, 0, :, 1], dh[1][:], relu_a[1], MULT)
         a_sb[2] = load_a(2, "dy_w")
         a_last = []
-        for r, (lo, hi) in enumerate(((0, T - CHUNK), (T - CHUNK, T))):
-            part = tile([P, hi - lo], F32, "a3_%d" % lo, relu_tags[r])
+        for lo, hi, tag in ((0, T - CHUNK, "a1"), (T - CHUNK, T, "relus")):
+            part = tile([P, hi - lo], F32, "a3_%d" % lo, tag)
             nc.sync.dma_start(part[:], a_rows[3][:, :, lo:hi])
             a_last.extend(part[:, at : at + CHUNK] for at in range(0, hi - lo, CHUNK))
 

@@ -26,7 +26,7 @@ PER_COLUMN = 16
 QUADRANTS = 4
 RUN = 8
 FIRST = 256
-SHARE = 576
+SHARE = 544
 OVERLAP = 16
 PIECE = 384
 CHUNK = 256

@@ -27,7 +27,6 @@ QUADRANTS = 4
 RUN = 8
 FIRST = 256
 SHARE = 544
-OVERLAP = 16
 PIECE = 384
 CHUNK = 256
 F32_MAX = 3.4028234663852886e38
@@ -81,7 +80,10 @@ def tile_moe_sub_relu2_kernel(
         w1_rows = w1t.rearrange("(b r c) n -> r b c n", r=PACK, c=RUN)
         for r in range(PACK):
             nc.sync.dma_start(w1_raw[:, r, :], w1_rows[r])
-        a_sb = {r: load_a(r) for r in (0, 1)}
+        a_sb = {}
+        a01 = tile([P, 2, T], F32, "a01")
+        for r in (0, 1):
+            nc.sync.dma_start(a01[:, r, :], a_rows[r])
 
         ring = tile([P, C + FIRST], U32, "g_w")
         g_w = [ring[:, FIRST : FIRST + C], ring[:, 0:C]]
@@ -176,14 +178,6 @@ def tile_moe_sub_relu2_kernel(
             weigh(second[r][:], r, 1, 0, C)
         weigh(rest[:], 0, 1, P, C)
         weigh(second[2][:], 2, 1, 0, C)
-        relus = tile([P, 2 * T - OVERLAP], F32, "relus")
-        relu_a = [relus[:, 0:T], relus[:, T - OVERLAP :]]
-
-        def relu(r, lo, hi):
-            nc.gpsimd.tensor_scalar(relu_a[r][:, lo:hi], a_sb[r][:, lo:hi], F32_MAX, 0.0, MIN, MAX)
-
-        relu(0, 0, T)
-        relu(1, OVERLAP, T)
 
         scatter_on_scalar(0, 0, FIRST)
         scatter_on_scalar(1, 0, T - 2 * PIECE)
@@ -198,6 +192,9 @@ def tile_moe_sub_relu2_kernel(
 
         w1_bf = tile([P, K, PACK], BF16, "w1_bf")
         nc.gpsimd.tensor_scalar(w1_bf[:], w1_raw[:].rearrange("p r k -> p k r"), 1.0, 0.0, MULT, ADD)
+        relus = tile([P, 2, T], F32, "relus")
+        nc.gpsimd.tensor_scalar(relus[:], a01[:], F32_MAX, 0.0, MIN, MAX)
+        relu_a = [relus[:, r, :] for r in (0, 1)]
         w1_w = tile([P, K], U32, "w1_w")
         w1_s = tile([P, K], U8, "w1_s")
         nc.vector.quantize_mx(
@@ -207,14 +204,12 @@ def tile_moe_sub_relu2_kernel(
         chunks = [slice(lo, lo + CHUNK) for lo in range(0, T, CHUNK)]
         pairs = tile([P, 2, T, 2], BF16, "pairs")
         nc.gpsimd.tensor_tensor(pairs[:, 0, :, 0], dh[0][:], relu_a[0], MULT)
-        relu(1, 0, OVERLAP)
         nc.gpsimd.tensor_tensor(pairs[:, 0, :, 1], dh[1][:], relu_a[1], MULT)
         a_sb[2] = load_a(2, "dy_w")
-        a_last = []
-        for lo, hi, tag in ((0, T - CHUNK, "a1"), (T - CHUNK, T, "relus")):
-            part = tile([P, hi - lo], F32, "a3_%d" % lo, tag)
-            nc.sync.dma_start(part[:], a_rows[3][:, :, lo:hi])
-            a_last.extend(part[:, at : at + CHUNK] for at in range(0, hi - lo, CHUNK))
+        a3 = tile([P, T], F32, "a3", "dh0")
+        for lo in (0, C):
+            nc.sync.dma_start(a3[:, lo : lo + C], a_rows[3][:, :, lo : lo + C])
+        a_last = [a3[:, cols] for cols in chunks]
 
         def multiply(r, cols, a_cols):
             nc.vector.scalar_tensor_tensor(pairs[:, 1, cols, r - 2], a_cols, 0.0, dh[r][:, cols], MAX, MULT)

@@ -218,7 +218,8 @@ def tile_moe_sub_relu2_kernel(
             da = tile([P, CHUNK, PACK], BF16, "da%d" % n)
             words = pairs[:].rearrange("p u t v -> p u (t v)").bitcast(F32)[:, :, chunks[n]]
             copy = nc.vector.tensor_copy if n == len(chunks) - 1 else nc.scalar.copy
-            copy(da[:].bitcast(F32), words.rearrange("p u t -> p t u"))
+            dst = da[:].bitcast(F32).rearrange("p (c i) u -> p c u i", i=4)
+            copy(dst, words.rearrange("p u (c i) -> p c u i", i=4))
             return da
 
         def quantize(n, da):

@@ -40,7 +40,11 @@ def tile_moe_sub_relu2_kernel(
     nc = tc.nc
     with ExitStack() as ctx:
         keep = ctx.enter_context(tc.tile_pool(name="keep", bufs=1))
+        apart = ctx.enter_context(tc.tile_pool(name="apart", bufs=1))
         psum = ctx.enter_context(tc.psum_pool(name="psum", bufs=1))
+
+        def placed(shape, name, kib, tag=None):
+            return apart.tile(shape, F32, name=name, tag=tag or name, align_bytes=ALIGN, offset=kib * 1024)
 
         def tile(shape, dtype, name, tag=None):
             return keep.tile(shape, dtype, name=name, tag=tag or name, align_bytes=ALIGN)
@@ -123,8 +127,8 @@ def tile_moe_sub_relu2_kernel(
             for n, r in enumerate(planes):
                 w2_s[e, r] = scales[n]
 
-        y_s = [tile([P, T], F32, "y_s%d" % r) for r in range(PACK)]
-        dh = [tile([P, 2 * T if r == 2 else T], F32, "dh%d" % r) for r in range(PACK)]
+        y_s = [placed([P, T], "y_s%d" % r, 32 * r) for r in range(PACK)]
+        dh = [placed([P, 2 * T if r == 2 else T], "dh%d" % r, 32 * r + 16) for r in range(PACK)]
 
 
         def bank(width):
@@ -206,7 +210,7 @@ def tile_moe_sub_relu2_kernel(
         nc.gpsimd.tensor_tensor(pairs[:, 0, :, 0], dh[0][:], relu_a[0], MULT)
         nc.gpsimd.tensor_tensor(pairs[:, 0, :, 1], dh[1][:], relu_a[1], MULT)
         a_sb[2] = load_a(2, "dy_w")
-        a3 = tile([P, T], F32, "a3", "dh0")
+        a3 = placed([P, T], "a3", 16, "dh0")
         for lo in (0, C):
             nc.sync.dma_start(a3[:, lo : lo + C], a_rows[3][:, :, lo : lo + C])
         a_last = [a3[:, cols] for cols in chunks]

from contextlib import ExitStack

import concourse.mybir as mybir

K, T, E, C, H, N = 256, 1024, 2, 512, 512, 512
FLOPS = 2 * N * H * E * C + 2 * H * K * T

F32 = mybir.dt.float32
BF16 = mybir.dt.bfloat16
I32 = mybir.dt.int32
U32 = mybir.dt.uint32
U16 = mybir.dt.uint16
U8 = mybir.dt.uint8
E4M3 = mybir.dt.float8_e4m3fn_x4
E5M2 = mybir.dt.float8_e5m2_x4
E2M1 = mybir.dt.float4_e2m1fn_x4
MULT = mybir.AluOpType.mult
ADD = mybir.AluOpType.add
MIN = mybir.AluOpType.min
MAX = mybir.AluOpType.max
COPY = mybir.ActivationFunctionType.Copy

P = 128
PACK = 4
PER_COLUMN = 16
QUADRANTS = 4
RUN = 8
FIRST = 256
SHARE = 544
PIECE = 384
CHUNK = 256
F32_MAX = 3.4028234663852886e38
ALIGN = 256
BANKS = 8


def tile_moe_sub_relu2_kernel(
    tc, dy_words, dy_scales, w2t_words, w2t_scales, w1t, a, gate, offs, out
):
    nc = tc.nc
    with ExitStack() as ctx:
        keep = ctx.enter_context(tc.tile_pool(name="keep", bufs=1))
        apart = ctx.enter_context(tc.tile_pool(name="apart", bufs=1))
        psum = ctx.enter_context(tc.psum_pool(name="psum", bufs=1))

        def placed(shape, name, kib, tag=None):
            return apart.tile(shape, F32, name=name, tag=tag or name, align_bytes=ALIGN, offset=kib * 1024)

        def tile(shape, dtype, name, tag=None):
            return keep.tile(shape, dtype, name=name, tag=tag or name, align_bytes=ALIGN)

        offsets = tile([P, T // PER_COLUMN], U16, "offsets")
        dy_w = tile([P, T], I32, "dy_w")
        dy_s = tile([P, T // 4], I32, "dy_s")
        w2_w_raw = [tile([P, H // 2], I32, "w2_w_raw%d" % e) for e in range(E)]
        w2_s_raw = tile([P, E, H // 4], I32, "w2_s_raw")
        gates = [tile([P, C], F32, "gate%d" % e) for e in range(E)]

        nc.gpsimd.memset(w2_s_raw[:], 0)

        nc.sync.dma_start(offsets[:], offs)
        dy_scale_rows = dy_scales[0].bitcast(I32)
        for q in range(QUADRANTS):
            queue = nc.sync if q < 2 else nc.scalar
            queue.dma_start(dy_s[32 * q : 32 * q + 32, :], dy_scale_rows[4 * q : 4 * q + 4, :].partition_broadcast(8))
        nc.sync.dma_start(dy_w[:], dy_words[0].rearrange("p t d -> p (t d)").bitcast(I32))
        nc.sync.dma_start(w2_w_raw[0][:], w2t_words[0, 0].bitcast(I32))
        nc.sync.dma_start(gates[0][:, 0:FIRST], gate[:, 0:FIRST])
        w2_scale_rows = w2t_scales[:, 0].rearrange("e b i -> b e i").bitcast(I32)
        for q in range(QUADRANTS):
            nc.sync.dma_start(w2_s_raw[32 * q : 32 * q + 4, :, :], w2_scale_rows[4 * q : 4 * q + 4, :, :])
        nc.sync.dma_start(gates[0][:, FIRST:C], gate[:, FIRST:C])
        nc.sync.dma_start(w2_w_raw[1][:], w2t_words[1, 0].bitcast(I32))
        nc.sync.dma_start(gates[1][:], gate[:, C:T])

        a_rows = a.rearrange("(b r c) n -> r b c n", r=PACK, c=RUN)

        def load_a(r, tag=None):
            plane = tile([P, T], F32, "a%d" % r, tag)
            nc.sync.dma_start(plane[:], a_rows[r])
            return plane

        w1_raw = tile([P, PACK, K], F32, "w1_raw")
        w1_rows = w1t.rearrange("(b r c) n -> r b c n", r=PACK, c=RUN)
        for r in range(PACK):
            nc.sync.dma_start(w1_raw[:, r, :], w1_rows[r])
        a_sb = {}
        a01 = tile([P, 2, T], F32, "a01")
        for r in (0, 1):
            nc.sync.dma_start(a01[:, r, :], a_rows[r])

        ring = tile([P, C + FIRST], U32, "g_w")
        g_w = [ring[:, FIRST : FIRST + C], ring[:, 0:C]]
        g_s = [tile([P, C], U8, "g_s0")]

        def slot_offsets(lo, hi):
            return offsets[:, lo // PER_COLUMN : hi // PER_COLUMN]

        def gather_scales(e):
            nc.vector.tensor_copy(g_s[e][:], dy_s[:].bitcast(U8).indirect(slot_offsets(e * C, (e + 1) * C)))

        def gather_words(e, lo, hi):
            window = dy_w[:].bitcast(U32).indirect(slot_offsets(e * C + lo, e * C + hi))
            nc.vector.tensor_copy(g_w[e][:, lo:hi], window)

        gather_scales(0)
        gather_words(0, 0, FIRST)
        gather_words(0, FIRST, C)
        gather_words(1, 0, FIRST)

        w2_w, w2_s = {}, {}
        sorters = (nc.scalar.copy, nc.gpsimd.tensor_copy)

        def sort_columns(name, copy, src, w, planes):
            dst = tile([P, len(planes), P // RUN, w], U32, name)
            src = src.bitcast(U32).rearrange("p (b r w) -> p r b w", r=PACK, w=w)
            copy(dst[:], src[:, planes[0] : planes[-1] + 1])
            return [dst[:, n].rearrange("p b w -> p (b w)").bitcast(U8) for n in range(len(planes))]

        def sort_words(e, planes):
            words = sort_columns("w2_w%d_%d" % (e, planes[0]), sorters[e], w2_w_raw[e][:], RUN // 2, planes)
            for n, r in enumerate(planes):
                w2_w[e, r] = words[n]

        def sort_scales(e, planes):
            scales = sort_columns("w2_s%d_%d" % (e, planes[0]), sorters[e], w2_s_raw[:, e, :], RUN // 4, planes)
            for n, r in enumerate(planes):
                w2_s[e, r] = scales[n]

        y_s = [placed([P, T], "y_s%d" % r, 32 * r) for r in range(PACK)]
        dh = [placed([P, 2 * T if r == 2 else T], "dh%d" % r, 32 * r + 16) for r in range(PACK)]


        def bank(width):
            return psum.tile([P, width], F32, name="acc", tag="acc", bufs=BANKS)

        def product(r, e, *edges):
            acc = bank(edges[-1] - edges[0])
            for lo, hi in zip(edges, edges[1:]):
                nc.tensor.matmul_mx(
                    out=acc[:, lo - edges[0] : hi - edges[0]],
                    lhsT=w2_w[e, r].bitcast(E2M1),
                    lhsT_scale=w2_s[e, r],
                    rhs=g_w[e][:, lo:hi].bitcast(E5M2),
                    rhs_scale=g_s[e][:, lo:hi],
                    start=True,
                    stop=True,
                )
            return acc

        def weigh(acc, r, e, lo, hi):
            dst = y_s[r][:, e * C + lo : e * C + hi]
            nc.vector.scalar_tensor_tensor(dst, acc, 2.0, gates[e][:, lo:hi], MULT, MULT)

        def scatter_on_scalar(r, lo, hi):
            nc.scalar.activation(dh[r][:].indirect(slot_offsets(lo, hi)), y_s[r][:, lo:hi], COPY)

        def scatter_on_vector(r, lo, hi):
            nc.vector.tensor_copy(dh[r][:].indirect(slot_offsets(lo, hi)), y_s[r][:, lo:hi])

        sort_words(0, [0])
        sort_words(0, [1, 2, 3])
        sort_scales(0, [0])
        sort_scales(0, [1, 2, 3])
        halves = [product(0, 0, lo, hi) for lo, hi in ((0, FIRST), (FIRST, C))]
        first = {r: product(r, 0, 0, C) for r in range(1, PACK)}
        weigh(halves[0][:], 0, 0, 0, FIRST)
        g_s.append(tile([P, C], U8, "g_s1", "w2_w0_0"))
        gather_scales(1)
        weigh(first[1][:], 1, 0, 0, C)
        gather_words(1, FIRST, C)
        weigh(halves[1][:], 0, 0, FIRST, C)
        sort_words(1, [0, 1, 2, 3])
        sort_scales(1, [0, 1, 2, 3])
        weigh(product(0, 1, 0, P)[:], 0, 1, 0, P)
        second = {r: product(r, 1, 0, C) for r in (1, 3)}
        rest = product(0, 1, P, FIRST, C)
        second[2] = product(2, 1, 0, C)
        for r in (3, 2):
            weigh(first[r][:], r, 0, 0, C)
        for r in (1, 3):
            weigh(second[r][:], r, 1, 0, C)
        weigh(rest[:], 0, 1, P, C)
        weigh(second[2][:], 2, 1, 0, C)

        scatter_on_scalar(0, 0, FIRST)
        scatter_on_scalar(1, 0, T - 2 * PIECE)
        scatter_on_scalar(0, FIRST, SHARE)
        scatter_on_scalar(1, T - 2 * PIECE, T - PIECE)
        scatter_on_scalar(3, 2 * PIECE, T)
        scatter_on_scalar(1, T - PIECE, T)
        scatter_on_scalar(3, 0, PIECE)
        scatter_on_scalar(3, PIECE, 2 * PIECE)
        scatter_on_vector(0, SHARE, T)
        scatter_on_vector(2, 0, T)

        w1_bf = tile([P, K, PACK], BF16, "w1_bf")
        nc.gpsimd.tensor_scalar(w1_bf[:], w1_raw[:].rearrange("p r k -> p k r"), 1.0, 0.0, MULT, ADD)
        relus = tile([P, 2, T], F32, "relus")
        nc.gpsimd.tensor_scalar(relus[:], a01[:], F32_MAX, 0.0, MIN, MAX)
        relu_a = [relus[:, r, :] for r in (0, 1)]
        w1_w = tile([P, K], U32, "w1_w")
        w1_s = tile([P, K], U8, "w1_s")
        nc.vector.quantize_mx(
            out=w1_w[:].bitcast(E4M3), scales=w1_s[:], in_=w1_bf[:].rearrange("p k r -> p (k r)")
        )

        chunks = [slice(lo, lo + CHUNK) for lo in range(0, T, CHUNK)]
        pairs = tile([P, 2, T, 2], BF16, "pairs")
        nc.gpsimd.tensor_tensor(pairs[:, 0, :, 0], dh[0][:], relu_a[0], MULT)
        nc.gpsimd.tensor_tensor(pairs[:, 0, :, 1], dh[1][:], relu_a[1], MULT)
        a_sb[2] = load_a(2, "dy_w")
        a3 = placed([P, T], "a3", 16, "dh0")
        for lo in (0, C):
            nc.sync.dma_start(a3[:, lo : lo + C], a_rows[3][:, :, lo : lo + C])
        a_last = [a3[:, cols] for cols in chunks]

        def multiply(r, cols, a_cols):
            nc.vector.scalar_tensor_tensor(pairs[:, 1, cols, r - 2], a_cols, 0.0, dh[r][:, cols], MAX, MULT)

        def weave(n):
            da = tile([P, CHUNK, PACK], BF16, "da%d" % n)
            words = pairs[:].rearrange("p u t v -> p u (t v)").bitcast(F32)[:, :, chunks[n]]
            copy = nc.vector.tensor_copy if n == len(chunks) - 1 else nc.scalar.copy
            dst = da[:].bitcast(F32).rearrange("p (c i) u -> p c u i", i=4)
            copy(dst, words.rearrange("p u (c i) -> p c u i", i=4))
            return da

        def quantize(n, da):
            da_w = tile([P, CHUNK], U32, "da_w%d" % n)
            da_s = tile([P, CHUNK], U8, "da_s%d" % n)
            nc.vector.quantize_mx(
                out=da_w[:].bitcast(E5M2), scales=da_s[:], in_=da[:].rearrange("p t r -> p (t r)")
            )
            accs = []
            for kt in range(K // P):
                rows = slice(kt * P, (kt + 1) * P)
                accs.append(bank(CHUNK))
                nc.tensor.matmul_mx(
                    out=accs[kt][:],
                    lhsT=w1_w[:, rows].bitcast(E4M3),
                    lhsT_scale=w1_s[:, rows],
                    rhs=da_w[:].bitcast(E5M2),
                    rhs_scale=da_s[:],
                    start=True,
                    stop=True,
                )
            return accs

        def store(n, kt, acc):
            res = tile([P, CHUNK], F32, "res%d_%d" % (n, kt))
            copy = nc.vector.tensor_copy if (n, kt) in ((1, 0), (3, 0)) else nc.scalar.copy
            copy(res[:], acc[:])
            nc.sync.dma_start(out[kt * P : (kt + 1) * P, chunks[n]], res[:])

        multiply(2, slice(0, T), a_sb[2][:])
        results = []
        for n in range(len(chunks)):
            multiply(3, chunks[n], a_last[n])
            results.append(quantize(n, weave(n)))
        for n, accs in enumerate(results):
            for kt, acc in enumerate(accs):
                store(n, kt, acc)
